import numpy as np
import ml_dtypes


def mxq(x, axis, fmt="e4m3"):
    dtype, down = {"e4m3": (ml_dtypes.float8_e4m3fn, 7), "e5m2": (ml_dtypes.float8_e5m2, 14)}[fmt]
    v = np.moveaxis(np.asarray(x, np.float32).astype(ml_dtypes.bfloat16).astype(np.float64), axis, -1)
    blocks = v.reshape(v.shape[:-1] + (-1, 32))
    amax = np.abs(blocks).max(-1, keepdims=True)
    byte = np.maximum(np.where(amax > 0, np.frexp(amax)[1] - 1 + 127, 0) - down, 1)
    scale = np.exp2(byte - 127.0)
    codes = (blocks / scale).astype(np.float32).astype(dtype).astype(np.float64)
    return np.moveaxis((codes * scale).reshape(v.shape), -1, axis)


WIDE = False


def mx_kscale(k):
    if not WIDE:
        return np.ones(k)
    levels = np.array([10, -10, 5, -5, 0])
    if k % 512:
        return np.exp2(np.random.permutation(np.resize(levels, k // 32))).repeat(32)
    a = np.empty((k // 512, 16))
    for p in range(k // 512):
        a[p, :8] = np.random.permutation(np.resize(levels, 8))
        for g in range(8):
            far = levels[np.abs(levels - a[p, g]) >= 10]
            a[p, g + 8] = far[np.random.randint(len(far))]
    return np.exp2(a.ravel()).repeat(32)


def f64(x):
    return np.asarray(x).astype(np.float64)


def striped(idx):
    return np.tile(idx.reshape(-1, 16).T, (8, 1)).astype(np.uint16)


def unstriped(offs):
    return offs[:16].T.reshape(-1).astype(np.int64)


def pack_weight(w):
    k, n = w.shape
    w = f64(np.asarray(w, np.float32).astype(ml_dtypes.bfloat16)).reshape(k // 32, 32, n)
    amax = np.abs(w).max(1)
    byte = np.clip(np.where(amax > 0, np.frexp(amax)[1] - 1 + 127 - 7, 1), 1, 254)
    scaled = (w * np.exp2(127.0 - byte)[:, None, :]).reshape(k, n).astype(np.float32)
    words = np.ascontiguousarray(scaled.reshape(k // 512, 128, 4, n).transpose(0, 1, 3, 2)).astype(ml_dtypes.float8_e4m3fn).view(np.uint8)
    return words, np.ascontiguousarray(byte.astype(np.uint8).reshape(k // 512, 16, n))


def unpack_weight(words, scales):
    g, p, n, _ = words.shape
    vals = np.ascontiguousarray(words).view(ml_dtypes.float8_e4m3fn).astype(np.float64) * np.repeat(np.exp2(scales.astype(np.float64) - 127.0), 8, axis=1)[..., None]
    return vals.transpose(0, 1, 3, 2).reshape(g * 512, n)


def relu(v):
    return np.maximum(v, 0.0)


K, T, S, V, D, N, H = 512, 2048, 1024, 512, 4, 256, 512
P = 2 ** 7


def setup_inputs():
    n = np.random.standard_normal
    s = mx_kscale(K)[:, None]
    u = mx_kscale(H)
    packed_xT = pack_weight(n((K, T)) * s)
    return {
        "x_words": packed_xT[0],
        "x_scales": packed_xT[1],
        "hT": (n((K, V)) / np.sqrt(K) / s).astype(np.float32),
        "qn": (np.tile(np.random.uniform(0.5, 1.5, T), (P, 1))).astype(np.float32),
        "own": (np.random.uniform(0.5, 1.5, (V, 1))).astype(np.float32),
        "idf": (np.random.uniform(0.5, 1.5, (H, 1)) * u[:, None]).astype(np.float32),
        "bag": (np.random.uniform(0.0, 1.0, (H, N)) ** 6 / 40 / u[:, None]).astype(np.float32),
        "offs": striped(np.random.permutation(T)[:S]),
    }


def reference(x_words, x_scales, hT, qn, own, idf, bag, offs):
    hTq = mxq(f64(hT), 0, "e4m3")
    xq = unpack_weight(x_words, x_scales)[:, unstriped(offs)]
    dd = np.sqrt(relu(f64(qn)[:1][:, unstriped(offs)] - (1.5 * (hTq.T @ xq)) + f64(own)) + 0.01)
    near = dd.reshape(len(dd), -1, D).min(axis=2)
    z = f64(idf) * near
    return mxq(f64(bag), 0, "e4m3").T @ mxq(z, 0, "e4m3")

@@ -1,0 +1,212 @@
+from contextlib import ExitStack
+
+import concourse.mybir as mybir
+from concourse.masks import make_identity
+
+K, T, S, V, D, N = 512, 2048, 1024, 512, 4, 256
+P = 128
+PACK = 4
+G = S // D
+BLOCKS = G // P
+HALF = V // 2
+H_PARTS = ((0, 96), (96, 128))
+
+F32 = mybir.dt.float32
+BF16 = mybir.dt.bfloat16
+I32 = mybir.dt.int32
+U32 = mybir.dt.uint32
+U16 = mybir.dt.uint16
+U8 = mybir.dt.uint8
+FP8X4 = mybir.dt.float8_e4m3fn_x4
+ALU = mybir.AluOpType
+ACT = mybir.ActivationFunctionType
+
+FLOPS = 2 * K * V * S + 2 * V * N * G
+BYTES = K * T + 16 * T + 4 * (K * V + T + 2 * V + V * N + N * G) + 2 * P * (S // 16)
+
+
+def tile_picked_yrwmd_dist_p_kernel(
+    tc, x_words, x_scales, hT, qn, own, idf, bag, offs, out
+):
+    nc = tc.nc
+    with ExitStack() as ctx:
+        sb = ctx.enter_context(tc.tile_pool(name="sb", bufs=1))
+        ps = ctx.enter_context(tc.psum_pool(name="ps", bufs=1))
+
+        offsets = sb.tile([P, S // 16], U16, name="offsets")
+        nc.sync.dma_start(offsets[:], offs)
+
+        norm_table = sb.tile([P, T], F32, name="norm_table", align_bytes=64)
+        nc.vector.memset(norm_table[0 : P - 1, :], 0.0)
+        nc.sync.dma_start(norm_table[P - 1 : P, :], qn[0:1, :])
+        scale_table = sb.tile([P, T], U8, name="scale_table", align_bytes=64)
+        for q in range(4):
+            nc.sync.dma_start(
+                scale_table[32 * q : 32 * (q + 1), :].bitcast(I32),
+                x_scales[0, 4 * q : 4 * q + 4, :].bitcast(I32).unsqueeze(0).to_broadcast([8, 4, T // 4]),
+            )
+
+        h_rows = hT.rearrange("(p j) t -> p j t", j=PACK)
+        h_raw = []
+        word_table = sb.tile([P, T], U32, name="word_table", align_bytes=64)
+        for part, (lo, hi) in enumerate(H_PARTS):
+            raw = sb.tile([P, PACK, PACK * (hi - lo)], F32, name="h_raw%d" % part, tag="h_raw%d" % part, align_bytes=64)
+            nc.sync.dma_start(raw[:], h_rows[:, :, PACK * lo : PACK * hi])
+            h_raw.append(raw)
+            if part == 0:
+                nc.sync.dma_start(
+                    word_table[:].bitcast(I32),
+                    x_words[0].rearrange("p c r -> p (c r)").bitcast(I32),
+                )
+        own_cols = sb.tile([P, PACK], F32, name="own_cols")
+        nc.sync.dma_start(own_cols[:], own.rearrange("(p j) o -> p (j o)", j=PACK))
+        idf_cols = sb.tile([P, PACK], F32, name="idf_cols")
+        nc.sync.dma_start(idf_cols[:], idf.rearrange("(p j) o -> p (j o)", j=PACK))
+        bag_raw = sb.tile([P, PACK, N], F32, name="bag_raw")
+        nc.sync.dma_start(bag_raw[:], bag.rearrange("(p j) m -> p j m", j=PACK))
+
+        one = sb.tile([P, 1], F32, name="one")
+        nc.gpsimd.memset(one[:], 1.0)
+        eps = sb.tile([P, 1], F32, name="eps")
+        nc.scalar.activation(eps[:], one[:], ACT.Sqrt, scale=1e-4)
+        identity = sb.tile([P, P], F32, name="identity")
+        make_identity(nc, identity[:])
+
+        picked_norms = sb.tile([P, S], F32, name="picked_norms", align_bytes=64)
+        nc.vector.tensor_copy(picked_norms[:], norm_table[:].indirect(offsets[:]))
+        def pick_scales(b, tag):
+            picked = sb.tile([P, S // BLOCKS], U8, name="picked_scales%d" % b, tag=tag, align_bytes=64)
+            nc.vector.tensor_copy(picked[:], scale_table[:].indirect(offsets[:, 32 * b : 32 * (b + 1)]))
+            by_member = sb.tile([P, D, P], U8, name="x_scale%d" % b, align_bytes=64)
+            nc.vector.tensor_copy(by_member[:], picked[:].rearrange("p (g d) -> p d g", d=D))
+            return by_member
+
+        x_scale = [pick_scales(0, "picked_scales0")]
+
+        h_bf = sb.tile([P, PACK, P, PACK], BF16, name="h_bf", tag="h_bf", align_bytes=64)
+        for part, (lo, hi) in enumerate(H_PARTS):
+            nc.scalar.copy(
+                h_bf[:, :, lo:hi, :].rearrange("p r m j -> p m r j"),
+                h_raw[part][:].rearrange("p j (m r) -> p m r j", r=PACK),
+            )
+        h_codes = sb.tile([P, V], U32, name="h_codes", align_bytes=64)
+        h_scale = sb.tile([P, V], U8, name="h_scale", align_bytes=64)
+        nc.vector.quantize_mx(
+            out=h_codes[:].bitcast(FP8X4),
+            scales=h_scale[:],
+            in_=h_bf[:].rearrange("p r m j -> p (r m j)"),
+        )
+
+        x_codes = []
+        for b in range(BLOCKS):
+            if b == 1:
+                x_scale.append(pick_scales(1, "h_bf"))
+            codes = sb.tile([P, D, P], U32, name="x_codes%d" % b, tag=("x_codes0", "h_raw1")[b], align_bytes=64)
+            nc.vector.tensor_copy(
+                codes[:].rearrange("p d g -> p g d"),
+                word_table[:].indirect(offsets[:, 32 * b : 32 * (b + 1)]),
+            )
+            x_codes.append(codes)
+
+        shifts = sb.tile([P, BLOCKS, D], F32, name="shifts", tag="h_raw0", align_bytes=64)
+        shift = []
+        for b in range(BLOCKS):
+            turned = ps.tile([P, D, P], F32, name="norms_turned%d" % b, tag="bank%d" % (6 + b))
+            members = picked_norms[:, 512 * b : 512 * (b + 1)].rearrange("p (g d) -> p d g", d=D)
+            for d in range(D):
+                nc.tensor.transpose(turned[:, d, :], members[:, d, :], identity[:])
+            cols = shifts[:, b, :]
+            nc.scalar.activation(cols, turned[:, :, P - 1], ACT.Copy, scale=-2.0 / 3.0)
+            shift.append(cols)
+
+        best = []
+        for b in range(BLOCKS):
+            dots = []
+            for d in range(D):
+                acc = ps.tile([P, V], F32, name="dots%d_%d" % (b, d), tag="bank%d" % (4 * b + d))
+                nc.tensor.matmul_mx(
+                    out=acc[:],
+                    lhsT=x_codes[b][:, d, :].bitcast(FP8X4),
+                    lhsT_scale=x_scale[b][:, d, :],
+                    rhs=h_codes[:].bitcast(FP8X4),
+                    rhs_scale=h_scale[:],
+                    start=True,
+                    stop=True,
+                )
+                dots.append(acc)
+            first = sb.tile([P, V], F32, name="run%d_0" % b)
+            nc.scalar.activation(first[:], dots[0][:], ACT.Identity, bias=shift[b][:, 0:1])
+            run = [first[:, 0:HALF], first[:, HALF:V]]
+            for d in range(1, D):
+                for half in range(2):
+                    nxt = sb.tile([P, HALF], F32, name="run%d_%d_%d" % (b, d, half), tag="run%d_%d_%d" % (b, d, half), align_bytes=64)
+                    nc.vector.scalar_tensor_tensor(
+                        nxt[:],
+                        dots[d][:, half * HALF : (half + 1) * HALF],
+                        shift[b][:, d : d + 1],
+                        run[half],
+                        ALU.add,
+                        ALU.max,
+                    )
+                    run[half] = nxt[:]
+            best.append(run)
+
+        bag_bf = sb.tile([P, N, PACK], BF16, name="bag_bf", align_bytes=64)
+        nc.scalar.copy(
+            bag_bf[:].rearrange("p (c i) j -> p c j i", i=4),
+            bag_raw[:].rearrange("p j (c i) -> p c j i", i=4),
+        )
+
+        bag_codes = sb.tile([P, N], U32, name="bag_codes", tag="run1_2_0", align_bytes=64)
+        bag_scale = sb.tile([P, N], U8, name="bag_scale", align_bytes=64)
+        nc.vector.quantize_mx(
+            out=bag_codes[:].bitcast(FP8X4),
+            scales=bag_scale[:],
+            in_=bag_bf[:].rearrange("p m j -> p (m j)"),
+        )
+
+        for b in range(BLOCKS):
+            clipped = sb.tile([P, PACK, P], F32, name="clipped%d" % b)
+            for half in range(2):
+                for i in range(2):
+                    r = 2 * half + i
+                    turned = ps.tile([P, P], F32, name="best_turned%d_%d" % (b, r), tag="bank%d" % r)
+                    nc.tensor.transpose(turned[:], best[b][half][:, i * P : (i + 1) * P], identity[:])
+                    nc.scalar.activation(
+                        clipped[:, r, :], turned[:], ACT.Relu, bias=own_cols[:, r : r + 1], scale=-1.5
+                    )
+            z_bf = sb.tile([P, P, PACK], BF16, name="z_bf%d" % b, tag=("run1_2_1", "z_bf1")[b], align_bytes=64)
+            for half in range(2):
+                docs = slice(64 * half, 64 * (half + 1))
+                near = sb.tile([P, 64, PACK], F32, name="near%d_%d" % (b, half))
+                nc.scalar.activation(
+                    near[:], clipped[:, :, docs].rearrange("p r g -> p g r"), ACT.Sqrt, bias=eps[:]
+                )
+                nc.vector.tensor_tensor(
+                    z_bf[:, docs, :], near[:], idf_cols[:].unsqueeze(1).to_broadcast([P, 64, PACK]), ALU.mult
+                )
+            z_codes = sb.tile([P, P], U32, name="z_codes%d" % b, align_bytes=64)
+            z_scale = sb.tile([P, P], U8, name="z_scale%d" % b, align_bytes=64)
+            nc.vector.quantize_mx(
+                out=z_codes[:].bitcast(FP8X4),
+                scales=z_scale[:],
+                in_=z_bf[:].rearrange("p g r -> p (g r)"),
+            )
+            for a in range(N // P):
+                sums = ps.tile([P, P], F32, name="sums%d_%d" % (b, a), tag="bank%d" % (4 + 2 * b + a))
+                nc.tensor.matmul_mx(
+                    out=sums[:],
+                    lhsT=bag_codes[:, a * P : (a + 1) * P].bitcast(FP8X4),
+                    lhsT_scale=bag_scale[:, a * P : (a + 1) * P],
+                    rhs=z_codes[:].bitcast(FP8X4),
+                    rhs_scale=z_scale[:],
+                    start=True,
+                    stop=True,
+                )
+                result = sb.tile([P, P], F32, name="result%d_%d" % (b, a))
+                if a == 0:
+                    nc.scalar.copy(result[:], sums[:])
+                    nc.scalar.dma_start(out[0:P, b * P : (b + 1) * P], result[:])
+                else:
+                    nc.vector.tensor_copy(result[:], sums[:])
+                    nc.sync.dma_start(out[P : 2 * P, b * P : (b + 1) * P], result[:])

@@ -74,14 +74,27 @@ def tile_picked_yrwmd_dist_p_kernel(
 
         picked_norms = sb.tile([P, S], F32, name="picked_norms", align_bytes=64)
         nc.vector.tensor_copy(picked_norms[:], norm_table[:].indirect(offsets[:]))
-        def pick_scales(b, tag):
-            picked = sb.tile([P, S // BLOCKS], U8, name="picked_scales%d" % b, tag=tag, align_bytes=64)
-            nc.vector.tensor_copy(picked[:], scale_table[:].indirect(offsets[:, 32 * b : 32 * (b + 1)]))
-            by_member = sb.tile([P, D, P], U8, name="x_scale%d" % b, align_bytes=64)
-            nc.vector.tensor_copy(by_member[:], picked[:].rearrange("p (g d) -> p d g", d=D))
+        member_norms = sb.tile([P, BLOCKS, 2 * D], F32, name="member_norms")
+        for b in range(BLOCKS):
+            nc.scalar.dma_start(
+                member_norms[:, b, 0:D],
+                picked_norms[P - 1 : P, 512 * b : 512 * (b + 1)].rearrange("o (g d) -> o g d", d=D),
+            )
+        shifts = sb.tile([P, BLOCKS, D], F32, name="shifts")
+        nc.gpsimd.tensor_scalar(shifts[:], member_norms[:, :, 0:D], -2.0 / 3.0, 0.0, ALU.mult, ALU.add)
+        shift = [shifts[:, b, :] for b in range(BLOCKS)]
+
+        picked_scales = sb.tile([P, S], U8, name="picked_scales", align_bytes=64)
+        nc.vector.tensor_copy(picked_scales[:], scale_table[:].indirect(offsets[:]))
+
+        def deal_scales(b, tag):
+            by_member = sb.tile([P, D, P], U8, name="x_scale%d" % b, tag=tag, align_bytes=64)
+            nc.vector.tensor_copy(
+                by_member[:], picked_scales[:, 512 * b : 512 * (b + 1)].rearrange("p (g d) -> p d g", d=D)
+            )
             return by_member
 
-        x_scale = [pick_scales(0, "picked_scales0")]
+        x_scale = [deal_scales(0, "x_scale0")]
 
         h_bf = sb.tile([P, PACK, P, PACK], BF16, name="h_bf", tag="h_bf", align_bytes=64)
         for part, (lo, hi) in enumerate(H_PARTS):
@@ -99,8 +112,6 @@ def tile_picked_yrwmd_dist_p_kernel(
 
         x_codes = []
         for b in range(BLOCKS):
-            if b == 1:
-                x_scale.append(pick_scales(1, "h_bf"))
             codes = sb.tile([P, D, P], U32, name="x_codes%d" % b, tag=("x_codes0", "h_raw1")[b], align_bytes=64)
             nc.vector.tensor_copy(
                 codes[:].rearrange("p d g -> p g d"),
@@ -108,16 +119,7 @@ def tile_picked_yrwmd_dist_p_kernel(
             )
             x_codes.append(codes)
 
-        shifts = sb.tile([P, BLOCKS, D], F32, name="shifts", tag="h_raw0", align_bytes=64)
-        shift = []
-        for b in range(BLOCKS):
-            turned = ps.tile([P, D, P], F32, name="norms_turned%d" % b, tag="bank%d" % (6 + b))
-            members = picked_norms[:, 512 * b : 512 * (b + 1)].rearrange("p (g d) -> p d g", d=D)
-            for d in range(D):
-                nc.tensor.transpose(turned[:, d, :], members[:, d, :], identity[:])
-            cols = shifts[:, b, :]
-            nc.scalar.activation(cols, turned[:, :, P - 1], ACT.Copy, scale=-2.0 / 3.0)
-            shift.append(cols)
+        x_scale.append(deal_scales(1, "h_bf"))
 
         best = []
         for b in range(BLOCKS):
@@ -134,22 +136,39 @@ def tile_picked_yrwmd_dist_p_kernel(
                     stop=True,
                 )
                 dots.append(acc)
-            first = sb.tile([P, V], F32, name="run%d_0" % b)
-            nc.scalar.activation(first[:], dots[0][:], ACT.Identity, bias=shift[b][:, 0:1])
-            run = [first[:, 0:HALF], first[:, HALF:V]]
-            for d in range(1, D):
+            run = []
+            for half in range(2):
+                first = sb.tile([P, HALF], F32, name="run%d_0_%d" % (b, half))
+                nc.scalar.activation(
+                    first[:], dots[0][:, half * HALF : (half + 1) * HALF], ACT.Identity, bias=shift[b][:, 0:1]
+                )
+                run.append(first)
+            for d in range(1, D - 1):
                 for half in range(2):
-                    nxt = sb.tile([P, HALF], F32, name="run%d_%d_%d" % (b, d, half), tag="run%d_%d_%d" % (b, d, half), align_bytes=64)
+                    tag = "run%d_%d_%d" % (b, d, half)
+                    nxt = sb.tile([P, HALF], F32, name=tag, tag=tag, align_bytes=64)
                     nc.vector.scalar_tensor_tensor(
                         nxt[:],
                         dots[d][:, half * HALF : (half + 1) * HALF],
                         shift[b][:, d : d + 1],
-                        run[half],
+                        run[half][:],
                         ALU.add,
                         ALU.max,
                     )
-                    run[half] = nxt[:]
-            best.append(run)
+                    run[half] = nxt
+            slots = []
+            for lo, hi in ((0, 2), (2, 3), (3, 4)):
+                last = sb.tile([P, hi - lo, P], F32, name="best%d_%d" % (b, lo))
+                nc.vector.scalar_tensor_tensor(
+                    last[:].rearrange("p r m -> p (r m)"),
+                    dots[D - 1][:, lo * P : hi * P],
+                    shift[b][:, D - 1 : D],
+                    run[lo // 2][:, (lo % 2) * P : (lo % 2 + hi - lo) * P],
+                    ALU.add,
+                    ALU.max,
+                )
+                slots.extend(last[:, i, :] for i in range(hi - lo))
+            best.append(slots)
 
         bag_bf = sb.tile([P, N, PACK], BF16, name="bag_bf", align_bytes=64)
         nc.scalar.copy(
@@ -167,14 +186,12 @@ def tile_picked_yrwmd_dist_p_kernel(
 
         for b in range(BLOCKS):
             clipped = sb.tile([P, PACK, P], F32, name="clipped%d" % b)
-            for half in range(2):
-                for i in range(2):
-                    r = 2 * half + i
-                    turned = ps.tile([P, P], F32, name="best_turned%d_%d" % (b, r), tag="bank%d" % r)
-                    nc.tensor.transpose(turned[:], best[b][half][:, i * P : (i + 1) * P], identity[:])
-                    nc.scalar.activation(
-                        clipped[:, r, :], turned[:], ACT.Relu, bias=own_cols[:, r : r + 1], scale=-1.5
-                    )
+            for r in range(PACK):
+                turned = ps.tile([P, P], F32, name="best_turned%d_%d" % (b, r), tag="bank%d" % r)
+                nc.tensor.transpose(turned[:], best[b][r], identity[:])
+                nc.scalar.activation(
+                    clipped[:, r, :], turned[:], ACT.Relu, bias=own_cols[:, r : r + 1], scale=-1.5
+                )
             z_bf = sb.tile([P, P, PACK], BF16, name="z_bf%d" % b, tag=("run1_2_1", "z_bf1")[b], align_bytes=64)
             for half in range(2):
                 docs = slice(64 * half, 64 * (half + 1))
@@ -204,9 +221,9 @@ def tile_picked_yrwmd_dist_p_kernel(
                     stop=True,
                 )
                 result = sb.tile([P, P], F32, name="result%d_%d" % (b, a))
-                if a == 0:
+                if (b, a) == (BLOCKS - 1, 0):
                     nc.scalar.copy(result[:], sums[:])
                     nc.scalar.dma_start(out[0:P, b * P : (b + 1) * P], result[:])
                 else:
                     nc.vector.tensor_copy(result[:], sums[:])
-                    nc.sync.dma_start(out[P : 2 * P, b * P : (b + 1) * P], result[:])
+                    nc.sync.dma_start(out[a * P : (a + 1) * P, b * P : (b + 1) * P], result[:])

@@ -37,18 +37,20 @@ def tile_picked_yrwmd_dist_p_kernel(
         nc.sync.dma_start(offsets[:], offs)
 
         norm_table = sb.tile([P, T], F32, name="norm_table", align_bytes=64)
-        nc.vector.memset(norm_table[0 : P - 1, :], 0.0)
-        nc.sync.dma_start(norm_table[P - 1 : P, :], qn[0:1, :])
+        nc.scalar.dma_start(norm_table[P - 1 : P, :], qn[0:1, :])
         scale_table = sb.tile([P, T], U8, name="scale_table", align_bytes=64)
+        nc.gpsimd.memset(scale_table[:].bitcast(I32), 0)
+        nc.vector.memset(norm_table[0 : P - 1, 0 : T // 2], 0.0)
+        nc.gpsimd.memset(norm_table[0 : P - 1, T // 2 : T], 0.0)
         for q in range(4):
             nc.sync.dma_start(
-                scale_table[32 * q : 32 * (q + 1), :].bitcast(I32),
-                x_scales[0, 4 * q : 4 * q + 4, :].bitcast(I32).unsqueeze(0).to_broadcast([8, 4, T // 4]),
+                scale_table[32 * q : 32 * q + 4, :].bitcast(I32),
+                x_scales[0, 4 * q : 4 * q + 4, :].bitcast(I32),
             )
 
         h_rows = hT.rearrange("(p j) t -> p j t", j=PACK)
         h_raw = []
-        word_table = sb.tile([P, T], U32, name="word_table", align_bytes=64)
+        word_table = sb.tile([P, T], U32, name="word_table", tag="word_table", align_bytes=64)
         for part, (lo, hi) in enumerate(H_PARTS):
             raw = sb.tile([P, PACK, PACK * (hi - lo)], F32, name="h_raw%d" % part, tag="h_raw%d" % part, align_bytes=64)
             nc.sync.dma_start(raw[:], h_rows[:, :, PACK * lo : PACK * hi])
@@ -80,9 +82,6 @@ def tile_picked_yrwmd_dist_p_kernel(
                 member_norms[:, b, 0:D],
                 picked_norms[P - 1 : P, 512 * b : 512 * (b + 1)].rearrange("o (g d) -> o g d", d=D),
             )
-        shifts = sb.tile([P, BLOCKS, D], F32, name="shifts")
-        nc.gpsimd.tensor_scalar(shifts[:], member_norms[:, :, 0:D], -2.0 / 3.0, 0.0, ALU.mult, ALU.add)
-        shift = [shifts[:, b, :] for b in range(BLOCKS)]
 
         picked_scales = sb.tile([P, S], U8, name="picked_scales", align_bytes=64)
         nc.vector.tensor_copy(picked_scales[:], scale_table[:].indirect(offsets[:]))
@@ -102,6 +101,9 @@ def tile_picked_yrwmd_dist_p_kernel(
                 h_bf[:, :, lo:hi, :].rearrange("p r m j -> p m r j"),
                 h_raw[part][:].rearrange("p j (m r) -> p m r j", r=PACK),
             )
+        shifts = sb.tile([P, BLOCKS, D], F32, name="shifts", tag="h_raw1", align_bytes=64)
+        nc.scalar.activation(shifts[:], member_norms[:, :, 0:D], ACT.Copy, scale=-2.0 / 3.0)
+        shift = [shifts[:, b, :] for b in range(BLOCKS)]
         h_codes = sb.tile([P, V], U32, name="h_codes", align_bytes=64)
         h_scale = sb.tile([P, V], U8, name="h_scale", align_bytes=64)
         nc.vector.quantize_mx(
@@ -112,14 +114,14 @@ def tile_picked_yrwmd_dist_p_kernel(
 
         x_codes = []
         for b in range(BLOCKS):
-            codes = sb.tile([P, D, P], U32, name="x_codes%d" % b, tag=("x_codes0", "h_raw1")[b], align_bytes=64)
+            codes = sb.tile([P, D, P], U32, name="x_codes%d" % b, tag=("x_codes0", "h_bf")[b], align_bytes=64)
             nc.vector.tensor_copy(
                 codes[:].rearrange("p d g -> p g d"),
                 word_table[:].indirect(offsets[:, 32 * b : 32 * (b + 1)]),
             )
             x_codes.append(codes)
 
-        x_scale.append(deal_scales(1, "h_bf"))
+        x_scale.append(deal_scales(1, "word_table"))
 
         best = []
         for b in range(BLOCKS):
@@ -184,6 +186,7 @@ def tile_picked_yrwmd_dist_p_kernel(
             in_=bag_bf[:].rearrange("p m j -> p (m j)"),
         )
 
+        z_mx = []
         for b in range(BLOCKS):
             clipped = sb.tile([P, PACK, P], F32, name="clipped%d" % b)
             for r in range(PACK):
@@ -209,21 +212,33 @@ def tile_picked_yrwmd_dist_p_kernel(
                 scales=z_scale[:],
                 in_=z_bf[:].rearrange("p g r -> p (g r)"),
             )
-            for a in range(N // P):
-                sums = ps.tile([P, P], F32, name="sums%d_%d" % (b, a), tag="bank%d" % (4 + 2 * b + a))
-                nc.tensor.matmul_mx(
-                    out=sums[:],
-                    lhsT=bag_codes[:, a * P : (a + 1) * P].bitcast(FP8X4),
-                    lhsT_scale=bag_scale[:, a * P : (a + 1) * P],
-                    rhs=z_codes[:].bitcast(FP8X4),
-                    rhs_scale=z_scale[:],
-                    start=True,
-                    stop=True,
-                )
-                result = sb.tile([P, P], F32, name="result%d_%d" % (b, a))
-                if (b, a) == (BLOCKS - 1, 0):
-                    nc.scalar.copy(result[:], sums[:])
-                    nc.scalar.dma_start(out[0:P, b * P : (b + 1) * P], result[:])
-                else:
-                    nc.vector.tensor_copy(result[:], sums[:])
-                    nc.sync.dma_start(out[a * P : (a + 1) * P, b * P : (b + 1) * P], result[:])
+            z_mx.append((z_codes, z_scale))
+
+        def weigh(target, a, b):
+            nc.tensor.matmul_mx(
+                out=target,
+                lhsT=bag_codes[:, a * P : (a + 1) * P].bitcast(FP8X4),
+                lhsT_scale=bag_scale[:, a * P : (a + 1) * P],
+                rhs=z_mx[b][0][:].bitcast(FP8X4),
+                rhs_scale=z_mx[b][1][:],
+                start=True,
+                stop=True,
+            )
+
+        sums = ps.tile([P, N // P, P], F32, name="sums_first", tag="bank4")
+        for a in range(N // P):
+            weigh(sums[:, a, :], a, 0)
+        result = sb.tile([P, N // P, P], F32, name="result_first")
+        nc.scalar.copy(result[:], sums[:])
+        nc.sync.dma_start(out.rearrange("(a p) g -> p a g", p=P)[:, :, 0:P], result[:])
+
+        upper = ps.tile([P, P], F32, name="sums_upper", tag="bank5")
+        weigh(upper[:], 0, 1)
+        lower = ps.tile([P, P], F32, name="sums_lower", tag="bank6")
+        weigh(lower[:], 1, 1)
+        upper_result = sb.tile([P, P], F32, name="upper_result")
+        nc.vector.tensor_copy(upper_result[:], upper[:])
+        nc.sync.dma_start(out[0:P, P : 2 * P], upper_result[:])
+        lower_result = sb.tile([P, P], F32, name="lower_result")
+        nc.scalar.copy(lower_result[:], lower[:])
+        nc.scalar.dma_start(out[P : 2 * P, P : 2 * P], lower_result[:])

@@ -9,7 +9,9 @@ PACK = 4
 G = S // D
 BLOCKS = G // P
 HALF = V // 2
-H_PARTS = ((0, 96), (96, 128))
+H_PARTS = ((0, 64), (64, 128))
+EPS = 0.01
+DOT_BANKS = ((0, 1, 2, 3), (4, 5, 0, 1))
 
 F32 = mybir.dt.float32
 BF16 = mybir.dt.bfloat16
@@ -36,11 +38,12 @@ def tile_picked_yrwmd_dist_p_kernel(
         offsets = sb.tile([P, S // 16], U16, name="offsets")
         nc.sync.dma_start(offsets[:], offs)
 
-        norm_table = sb.tile([P, T], F32, name="norm_table", align_bytes=64)
+        norm_table = sb.tile([P, T], F32, name="norm_table", tag="norm_table", align_bytes=64)
         nc.scalar.dma_start(norm_table[P - 1 : P, :], qn[0:1, :])
         scale_table = sb.tile([P, T], U8, name="scale_table", align_bytes=64)
         nc.gpsimd.memset(scale_table[:].bitcast(I32), 0)
-        nc.vector.memset(norm_table[0 : P - 1, 0 : T // 2], 0.0)
+        nc.vector.memset(norm_table[0 : P - 1, 0 : T // 2 - 1], 0.0)
+        nc.vector.memset(norm_table[0 : P - 1, T // 2 - 1 : T // 2], 0.0)
         nc.gpsimd.memset(norm_table[0 : P - 1, T // 2 : T], 0.0)
         for q in range(4):
             nc.sync.dma_start(
@@ -50,40 +53,41 @@ def tile_picked_yrwmd_dist_p_kernel(
 
         h_rows = hT.rearrange("(p j) t -> p j t", j=PACK)
         h_raw = []
-        word_table = sb.tile([P, T], U32, name="word_table", tag="word_table", align_bytes=64)
         for part, (lo, hi) in enumerate(H_PARTS):
             raw = sb.tile([P, PACK, PACK * (hi - lo)], F32, name="h_raw%d" % part, tag="h_raw%d" % part, align_bytes=64)
             nc.sync.dma_start(raw[:], h_rows[:, :, PACK * lo : PACK * hi])
             h_raw.append(raw)
-            if part == 0:
-                nc.sync.dma_start(
-                    word_table[:].bitcast(I32),
-                    x_words[0].rearrange("p c r -> p (c r)").bitcast(I32),
-                )
         own_cols = sb.tile([P, PACK], F32, name="own_cols")
         nc.sync.dma_start(own_cols[:], own.rearrange("(p j) o -> p (j o)", j=PACK))
         idf_cols = sb.tile([P, PACK], F32, name="idf_cols")
         nc.sync.dma_start(idf_cols[:], idf.rearrange("(p j) o -> p (j o)", j=PACK))
-        bag_raw = sb.tile([P, PACK, N], F32, name="bag_raw")
-        nc.sync.dma_start(bag_raw[:], bag.rearrange("(p j) m -> p j m", j=PACK))
+        word_table = sb.tile([P, T], U32, name="word_table", tag="word_table", align_bytes=64)
+        nc.sync.dma_start(
+            word_table[:].bitcast(I32),
+            x_words[0].rearrange("p c r -> p (c r)").bitcast(I32),
+        )
 
         one = sb.tile([P, 1], F32, name="one")
         nc.gpsimd.memset(one[:], 1.0)
         eps = sb.tile([P, 1], F32, name="eps")
-        nc.scalar.activation(eps[:], one[:], ACT.Sqrt, scale=1e-4)
+        nc.scalar.activation(eps[:], one[:], ACT.Sqrt, scale=EPS * EPS)
+        ceiling = sb.tile([P, 1], F32, name="ceiling")
+        nc.scalar.activation(ceiling[:], eps[:], ACT.Copy, scale=-2.0 / 3.0)
         identity = sb.tile([P, P], F32, name="identity")
         make_identity(nc, identity[:])
 
         picked_norms = sb.tile([P, S], F32, name="picked_norms", align_bytes=64)
         nc.vector.tensor_copy(picked_norms[:], norm_table[:].indirect(offsets[:]))
-        member_norms = sb.tile([P, BLOCKS, 2 * D], F32, name="member_norms")
+        member_norms = sb.tile([P, BLOCKS, 2 * D], F32, name="member_norms", align_bytes=64)
         for b in range(BLOCKS):
-            nc.scalar.dma_start(
+            nc.sync.dma_start(
                 member_norms[:, b, 0:D],
                 picked_norms[P - 1 : P, 512 * b : 512 * (b + 1)].rearrange("o (g d) -> o g d", d=D),
             )
+        bag_raw = sb.tile([P, PACK, N], F32, name="bag_raw", tag="norm_table", align_bytes=64)
+        nc.sync.dma_start(bag_raw[:], bag.rearrange("(p j) m -> p j m", j=PACK))
 
-        picked_scales = sb.tile([P, S], U8, name="picked_scales", align_bytes=64)
+        picked_scales = sb.tile([P, S], U8, name="picked_scales", tag="picked_scales", align_bytes=64)
         nc.vector.tensor_copy(picked_scales[:], scale_table[:].indirect(offsets[:]))
 
         def deal_scales(b, tag):
@@ -101,8 +105,8 @@ def tile_picked_yrwmd_dist_p_kernel(
                 h_bf[:, :, lo:hi, :].rearrange("p r m j -> p m r j"),
                 h_raw[part][:].rearrange("p j (m r) -> p m r j", r=PACK),
             )
-        shifts = sb.tile([P, BLOCKS, D], F32, name="shifts", tag="h_raw1", align_bytes=64)
-        nc.scalar.activation(shifts[:], member_norms[:, :, 0:D], ACT.Copy, scale=-2.0 / 3.0)
+        shifts = sb.tile([P, BLOCKS, D], F32, name="shifts")
+        nc.scalar.activation(shifts[:], member_norms[:, :, 0:D], ACT.Copy, scale=-2.0 / 3.0, bias=-EPS / 1.5)
         shift = [shifts[:, b, :] for b in range(BLOCKS)]
         h_codes = sb.tile([P, V], U32, name="h_codes", align_bytes=64)
         h_scale = sb.tile([P, V], U8, name="h_scale", align_bytes=64)
@@ -123,11 +127,45 @@ def tile_picked_yrwmd_dist_p_kernel(
 
         x_scale.append(deal_scales(1, "word_table"))
 
+        idf_squared = sb.tile([P, PACK], F32, name="idf_squared", tag="idf_squared", align_bytes=64)
+        nc.gpsimd.tensor_tensor(idf_squared[:], idf_cols[:], idf_cols[:], ALU.mult)
+        idf_positive = sb.tile([P, PACK], F32, name="idf_positive")
+        nc.gpsimd.tensor_scalar(idf_positive[:], idf_cols[:], 0.0, None, ALU.is_ge)
+        idf_sign = sb.tile([P, PACK], F32, name="idf_sign")
+        nc.gpsimd.tensor_scalar(idf_sign[:], idf_positive[:], 2.0, -1.0, ALU.mult, ALU.add)
+        idf_size = sb.tile([P, PACK], F32, name="idf_size")
+        nc.gpsimd.tensor_tensor(idf_size[:], idf_cols[:], idf_sign[:], ALU.mult)
+
+        own_spread = ps.tile([P, PACK, P], F32, name="own_spread", tag="bank5")
+        for r in range(PACK):
+            nc.tensor.transpose(own_spread[:, r, :], own_cols[:, r : r + 1].to_broadcast([P, P]), identity[:])
+        own_rows = sb.tile([P, PACK, P], F32, name="own_rows")
+        nc.scalar.activation(own_rows[:], own_spread[:], ACT.Copy, scale=-2.0 / 3.0)
+
+        bag_bf = sb.tile([P, N, PACK], BF16, name="bag_bf", tag="picked_scales", align_bytes=64)
+        for quarter in range(4):
+            cols = slice(64 * quarter, 64 * (quarter + 1))
+            nc.gpsimd.tensor_tensor(
+                bag_bf[:, cols, :],
+                bag_raw[:, :, cols].rearrange("p j m -> p m j"),
+                idf_sign[:].unsqueeze(1).to_broadcast([P, 64, PACK]),
+                ALU.mult,
+            )
+
+        turned = []
+        for b in range(BLOCKS):
+            bank = ps.tile([P, PACK, P], F32, name="turned%d" % b, tag="bank%d" % (6 + b))
+            for r in range(PACK):
+                nc.tensor.matmul(
+                    bank[:, r, :], own_rows[:, r, :], identity[:], start=(r == 0), stop=False, is_transpose=True
+                )
+            turned.append(bank)
+
         best = []
         for b in range(BLOCKS):
             dots = []
             for d in range(D):
-                acc = ps.tile([P, V], F32, name="dots%d_%d" % (b, d), tag="bank%d" % (4 * b + d))
+                acc = ps.tile([P, V], F32, name="dots%d_%d" % (b, d), tag="bank%d" % DOT_BANKS[b][d])
                 nc.tensor.matmul_mx(
                     out=acc[:],
                     lhsT=x_codes[b][:, d, :].bitcast(FP8X4),
@@ -140,15 +178,17 @@ def tile_picked_yrwmd_dist_p_kernel(
                 dots.append(acc)
             run = []
             for half in range(2):
-                first = sb.tile([P, HALF], F32, name="run%d_0_%d" % (b, half))
+                tag = "run%d_0_%d" % (b, half)
+                first = sb.tile([P, HALF], F32, name="run%d_0_%d" % (b, half), tag=tag, align_bytes=64)
                 nc.scalar.activation(
                     first[:], dots[0][:, half * HALF : (half + 1) * HALF], ACT.Identity, bias=shift[b][:, 0:1]
                 )
                 run.append(first)
             for d in range(1, D - 1):
                 for half in range(2):
-                    tag = "run%d_%d_%d" % (b, d, half)
-                    nxt = sb.tile([P, HALF], F32, name=tag, tag=tag, align_bytes=64)
+                    name = "run%d_%d_%d" % (b, d, half)
+                    tag = "run0_2_%d" % half if (b, d) == (1, 1) else name
+                    nxt = sb.tile([P, HALF], F32, name=name, tag=tag, align_bytes=64)
                     nc.vector.scalar_tensor_tensor(
                         nxt[:],
                         dots[d][:, half * HALF : (half + 1) * HALF],
@@ -159,7 +199,7 @@ def tile_picked_yrwmd_dist_p_kernel(
                     )
                     run[half] = nxt
             slots = []
-            for lo, hi in ((0, 2), (2, 3), (3, 4)):
+            for lo, hi in (((0, 2), (2, 4)), ((0, 2), (2, 3), (3, 4)))[b]:
                 last = sb.tile([P, hi - lo, P], F32, name="best%d_%d" % (b, lo))
                 nc.vector.scalar_tensor_tensor(
                     last[:].rearrange("p r m -> p (r m)"),
@@ -172,13 +212,13 @@ def tile_picked_yrwmd_dist_p_kernel(
                 slots.extend(last[:, i, :] for i in range(hi - lo))
             best.append(slots)
 
-        bag_bf = sb.tile([P, N, PACK], BF16, name="bag_bf", align_bytes=64)
-        nc.scalar.copy(
-            bag_bf[:].rearrange("p (c i) j -> p c j i", i=4),
-            bag_raw[:].rearrange("p j (c i) -> p c j i", i=4),
-        )
+        for b in range(BLOCKS):
+            for r in range(PACK):
+                nc.tensor.matmul(
+                    turned[b][:, r, :], best[b][r], identity[:], start=False, stop=(r == PACK - 1), is_transpose=True
+                )
 
-        bag_codes = sb.tile([P, N], U32, name="bag_codes", tag="run1_2_0", align_bytes=64)
+        bag_codes = sb.tile([P, N], U32, name="bag_codes", tag="run1_2_1", align_bytes=64)
         bag_scale = sb.tile([P, N], U8, name="bag_scale", align_bytes=64)
         nc.vector.quantize_mx(
             out=bag_codes[:].bitcast(FP8X4),
@@ -186,31 +226,50 @@ def tile_picked_yrwmd_dist_p_kernel(
             in_=bag_bf[:].rearrange("p m j -> p (m j)"),
         )
 
-        z_mx = []
+        z_bf = []
         for b in range(BLOCKS):
-            clipped = sb.tile([P, PACK, P], F32, name="clipped%d" % b)
-            for r in range(PACK):
-                turned = ps.tile([P, P], F32, name="best_turned%d_%d" % (b, r), tag="bank%d" % r)
-                nc.tensor.transpose(turned[:], best[b][r], identity[:])
-                nc.scalar.activation(
-                    clipped[:, r, :], turned[:], ACT.Relu, bias=own_cols[:, r : r + 1], scale=-1.5
-                )
-            z_bf = sb.tile([P, P, PACK], BF16, name="z_bf%d" % b, tag=("run1_2_1", "z_bf1")[b], align_bytes=64)
+            clipped = sb.tile([P, P, PACK], F32, name="clipped%d" % b, align_bytes=64)
+            rounded = sb.tile([P, P, PACK], BF16, name="z_bf%d" % b, align_bytes=64)
             for half in range(2):
                 docs = slice(64 * half, 64 * (half + 1))
-                near = sb.tile([P, 64, PACK], F32, name="near%d_%d" % (b, half))
-                nc.scalar.activation(
-                    near[:], clipped[:, :, docs].rearrange("p r g -> p g r"), ACT.Sqrt, bias=eps[:]
-                )
-                nc.vector.tensor_tensor(
-                    z_bf[:, docs, :], near[:], idf_cols[:].unsqueeze(1).to_broadcast([P, 64, PACK]), ALU.mult
-                )
-            z_codes = sb.tile([P, P], U32, name="z_codes%d" % b, align_bytes=64)
+                if b == 0:
+                    near = sb.tile([P, 64, PACK], F32, name="near%d" % half, align_bytes=64)
+                    nc.scalar.activation(
+                        clipped[:, docs, :],
+                        turned[b][:, :, docs].rearrange("p r g -> p g r"),
+                        ACT.Relu,
+                        scale=-1.5,
+                        bias=-EPS,
+                    )
+                    nc.scalar.activation(near[:], clipped[:, docs, :], ACT.Sqrt, bias=eps[:])
+                    nc.gpsimd.tensor_tensor(
+                        rounded[:, docs, :],
+                        near[:],
+                        idf_size[:].unsqueeze(1).to_broadcast([P, 64, PACK]),
+                        ALU.mult,
+                    )
+                else:
+                    nc.vector.scalar_tensor_tensor(
+                        clipped[:, docs, :],
+                        turned[b][:, :, docs].rearrange("p r g -> p g r"),
+                        ceiling[:],
+                        idf_squared[:].unsqueeze(1).to_broadcast([P, 64, PACK]),
+                        ALU.min,
+                        ALU.mult,
+                    )
+                    nc.scalar.activation(rounded[:, docs, :], clipped[:, docs, :], ACT.Sqrt, scale=-1.5)
+            z_bf.append(rounded)
+
+        z_mx = []
+        for b in range(BLOCKS):
+            z_codes = sb.tile(
+                [P, P], U32, name="z_codes%d" % b, tag=("idf_squared", "z_codes1")[b], align_bytes=64
+            )
             z_scale = sb.tile([P, P], U8, name="z_scale%d" % b, align_bytes=64)
             nc.vector.quantize_mx(
                 out=z_codes[:].bitcast(FP8X4),
                 scales=z_scale[:],
-                in_=z_bf[:].rearrange("p g r -> p (g r)"),
+                in_=z_bf[b][:].rearrange("p g r -> p (g r)"),
             )
             z_mx.append((z_codes, z_scale))
 
@@ -225,16 +284,16 @@ def tile_picked_yrwmd_dist_p_kernel(
                 stop=True,
             )
 
-        sums = ps.tile([P, N // P, P], F32, name="sums_first", tag="bank4")
+        sums = ps.tile([P, N // P, P], F32, name="sums_first", tag="bank2")
         for a in range(N // P):
             weigh(sums[:, a, :], a, 0)
         result = sb.tile([P, N // P, P], F32, name="result_first")
         nc.scalar.copy(result[:], sums[:])
         nc.sync.dma_start(out.rearrange("(a p) g -> p a g", p=P)[:, :, 0:P], result[:])
 
-        upper = ps.tile([P, P], F32, name="sums_upper", tag="bank5")
+        upper = ps.tile([P, P], F32, name="sums_upper", tag="bank3")
         weigh(upper[:], 0, 1)
-        lower = ps.tile([P, P], F32, name="sums_lower", tag="bank6")
+        lower = ps.tile([P, P], F32, name="sums_lower", tag="bank4")
         weigh(lower[:], 1, 1)
         upper_result = sb.tile([P, P], F32, name="upper_result")
         nc.vector.tensor_copy(upper_result[:], upper[:])

@@ -40,7 +40,7 @@ def tile_picked_yrwmd_dist_p_kernel(
 
         norm_table = sb.tile([P, T], F32, name="norm_table", tag="norm_table", align_bytes=64)
         nc.scalar.dma_start(norm_table[P - 1 : P, :], qn[0:1, :])
-        scale_table = sb.tile([P, T], U8, name="scale_table", align_bytes=64)
+        scale_table = sb.tile([P, T], U8, name="scale_table", tag="scale_table", align_bytes=64)
         nc.gpsimd.memset(scale_table[:].bitcast(I32), 0)
         nc.vector.memset(norm_table[0 : P - 1, 0 : T // 2 - 1], 0.0)
         nc.vector.memset(norm_table[0 : P - 1, T // 2 - 1 : T // 2], 0.0)
@@ -57,7 +57,7 @@ def tile_picked_yrwmd_dist_p_kernel(
             raw = sb.tile([P, PACK, PACK * (hi - lo)], F32, name="h_raw%d" % part, tag="h_raw%d" % part, align_bytes=64)
             nc.sync.dma_start(raw[:], h_rows[:, :, PACK * lo : PACK * hi])
             h_raw.append(raw)
-        own_cols = sb.tile([P, PACK], F32, name="own_cols")
+        own_cols = sb.tile([P, PACK], F32, name="own_cols", tag="own_cols", align_bytes=64)
         nc.sync.dma_start(own_cols[:], own.rearrange("(p j) o -> p (j o)", j=PACK))
         idf_cols = sb.tile([P, PACK], F32, name="idf_cols")
         nc.sync.dma_start(idf_cols[:], idf.rearrange("(p j) o -> p (j o)", j=PACK))
@@ -76,19 +76,21 @@ def tile_picked_yrwmd_dist_p_kernel(
         identity = sb.tile([P, P], F32, name="identity")
         make_identity(nc, identity[:])
 
-        picked_norms = sb.tile([P, S], F32, name="picked_norms", align_bytes=64)
-        nc.vector.tensor_copy(picked_norms[:], norm_table[:].indirect(offsets[:]))
-        member_norms = sb.tile([P, BLOCKS, 2 * D], F32, name="member_norms", align_bytes=64)
-        for b in range(BLOCKS):
-            nc.sync.dma_start(
-                member_norms[:, b, 0:D],
-                picked_norms[P - 1 : P, 512 * b : 512 * (b + 1)].rearrange("o (g d) -> o g d", d=D),
-            )
-        bag_raw = sb.tile([P, PACK, N], F32, name="bag_raw", tag="norm_table", align_bytes=64)
-        nc.sync.dma_start(bag_raw[:], bag.rearrange("(p j) m -> p j m", j=PACK))
+        def move_norms(b, picked_norms):
+            member_norms = sb.tile([P, D], F32, name="member_norms%d" % b, align_bytes=64)
+            nc.sync.dma_start(member_norms[:], picked_norms[P - 1 : P, :].rearrange("o (g d) -> o g d", d=D))
+            return member_norms
+
+        first_norms = sb.tile([P, D * P], F32, name="first_norms", align_bytes=64)
+        nc.vector.tensor_scalar(
+            first_norms[:], norm_table[:].indirect(offsets[:, 0:32]), -2.0 / 3.0, -EPS / 1.5, ALU.mult, ALU.add
+        )
+        shift = [move_norms(0, first_norms)]
 
         picked_scales = sb.tile([P, S], U8, name="picked_scales", tag="picked_scales", align_bytes=64)
         nc.vector.tensor_copy(picked_scales[:], scale_table[:].indirect(offsets[:]))
+        bag_raw = sb.tile([P, PACK, N], F32, name="bag_raw", tag="scale_table", align_bytes=64)
+        nc.sync.dma_start(bag_raw[:], bag.rearrange("(p j) m -> p j m", j=PACK))
 
         def deal_scales(b, tag):
             by_member = sb.tile([P, D, P], U8, name="x_scale%d" % b, tag=tag, align_bytes=64)
@@ -105,9 +107,6 @@ def tile_picked_yrwmd_dist_p_kernel(
                 h_bf[:, :, lo:hi, :].rearrange("p r m j -> p m r j"),
                 h_raw[part][:].rearrange("p j (m r) -> p m r j", r=PACK),
             )
-        shifts = sb.tile([P, BLOCKS, D], F32, name="shifts")
-        nc.scalar.activation(shifts[:], member_norms[:, :, 0:D], ACT.Copy, scale=-2.0 / 3.0, bias=-EPS / 1.5)
-        shift = [shifts[:, b, :] for b in range(BLOCKS)]
         h_codes = sb.tile([P, V], U32, name="h_codes", align_bytes=64)
         h_scale = sb.tile([P, V], U8, name="h_scale", align_bytes=64)
         nc.vector.quantize_mx(
@@ -141,6 +140,11 @@ def tile_picked_yrwmd_dist_p_kernel(
             nc.tensor.transpose(own_spread[:, r, :], own_cols[:, r : r + 1].to_broadcast([P, P]), identity[:])
         own_rows = sb.tile([P, PACK, P], F32, name="own_rows")
         nc.scalar.activation(own_rows[:], own_spread[:], ACT.Copy, scale=-2.0 / 3.0)
+        second_norms = sb.tile([P, D * P], F32, name="second_norms", tag="own_cols", align_bytes=64)
+        nc.scalar.activation(
+            second_norms[:], norm_table[:].indirect(offsets[:, 32:64]), ACT.Copy, scale=-2.0 / 3.0, bias=-EPS / 1.5
+        )
+        shift.append(move_norms(1, second_norms))
 
         bag_bf = sb.tile([P, N, PACK], BF16, name="bag_bf", tag="picked_scales", align_bytes=64)
         for quarter in range(4):

@@ -11,7 +11,9 @@ BLOCKS = G // P
 HALF = V // 2
 H_PARTS = ((0, 64), (64, 128))
 EPS = 0.01
-DOT_BANKS = ((0, 1, 2, 3), (4, 5, 0, 1))
+SCALE_ROWS = 16
+FACTOR_AT = 2 * PACK * V
+DOT_BANKS = ((0, 1, 2, 3), (0, 1, 2, 1))
 
 F32 = mybir.dt.float32
 BF16 = mybir.dt.bfloat16
@@ -33,81 +35,98 @@ def tile_picked_yrwmd_dist_p_kernel(
     nc = tc.nc
     with ExitStack() as ctx:
         sb = ctx.enter_context(tc.tile_pool(name="sb", bufs=1))
+        shared = ctx.enter_context(tc.tile_pool(name="shared", bufs=1))
         ps = ctx.enter_context(tc.psum_pool(name="ps", bufs=1))
 
         offsets = sb.tile([P, S // 16], U16, name="offsets")
         nc.sync.dma_start(offsets[:], offs)
 
-        norm_table = sb.tile([P, T], F32, name="norm_table", tag="norm_table", align_bytes=64)
+        norm_table = sb.tile([P, T], F32, name="norm_table", align_bytes=64)
         nc.scalar.dma_start(norm_table[P - 1 : P, :], qn[0:1, :])
         scale_table = sb.tile([P, T], U8, name="scale_table", tag="scale_table", align_bytes=64)
-        nc.gpsimd.memset(scale_table[:].bitcast(I32), 0)
-        nc.vector.memset(norm_table[0 : P - 1, 0 : T // 2 - 1], 0.0)
-        nc.vector.memset(norm_table[0 : P - 1, T // 2 - 1 : T // 2], 0.0)
-        nc.gpsimd.memset(norm_table[0 : P - 1, T // 2 : T], 0.0)
-        for q in range(4):
-            nc.sync.dma_start(
-                scale_table[32 * q : 32 * q + 4, :].bitcast(I32),
-                x_scales[0, 4 * q : 4 * q + 4, :].bitcast(I32),
-            )
-
+        nc.sync.dma_start(scale_table[P - SCALE_ROWS : P, :].bitcast(I32), x_scales[0].bitcast(I32))
+        own_cols = sb.tile([P, PACK], F32, name="own_cols")
+        nc.sync.dma_start(own_cols[:], own.rearrange("(p j) o -> p (j o)", j=PACK))
         h_rows = hT.rearrange("(p j) t -> p j t", j=PACK)
         h_raw = []
-        for part, (lo, hi) in enumerate(H_PARTS):
-            raw = sb.tile([P, PACK, PACK * (hi - lo)], F32, name="h_raw%d" % part, tag="h_raw%d" % part, align_bytes=64)
-            nc.sync.dma_start(raw[:], h_rows[:, :, PACK * lo : PACK * hi])
+        for part in range(2):
+            raw = sb.tile([P, PACK, HALF], F32, name="h_raw%d" % part, tag="h_raw%d" % part, align_bytes=64)
+            nc.sync.dma_start(raw[:], h_rows[:, :, HALF * part : HALF * (part + 1)])
             h_raw.append(raw)
-        own_cols = sb.tile([P, PACK], F32, name="own_cols", tag="own_cols", align_bytes=64)
-        nc.sync.dma_start(own_cols[:], own.rearrange("(p j) o -> p (j o)", j=PACK))
-        idf_cols = sb.tile([P, PACK], F32, name="idf_cols")
-        nc.sync.dma_start(idf_cols[:], idf.rearrange("(p j) o -> p (j o)", j=PACK))
         word_table = sb.tile([P, T], U32, name="word_table", tag="word_table", align_bytes=64)
         nc.sync.dma_start(
             word_table[:].bitcast(I32),
             x_words[0].rearrange("p c r -> p (c r)").bitcast(I32),
         )
+        bag_raw = sb.tile([P, PACK, N], F32, name="bag_raw", align_bytes=64)
+        nc.sync.dma_start(bag_raw[:], bag.rearrange("(p j) m -> p j m", j=PACK))
+        idf_cols = sb.tile([P, PACK], F32, name="idf_cols")
+        nc.sync.dma_start(idf_cols[:], idf.rearrange("(p j) o -> p (j o)", j=PACK))
 
         one = sb.tile([P, 1], F32, name="one")
-        nc.gpsimd.memset(one[:], 1.0)
+        nc.vector.memset(one[:], 1.0)
+        nc.gpsimd.memset(scale_table[0 : P - SCALE_ROWS, :].bitcast(I32), 0)
+        nc.vector.memset(norm_table[0 : P - 1, :], 0.0)
         eps = sb.tile([P, 1], F32, name="eps")
         nc.scalar.activation(eps[:], one[:], ACT.Sqrt, scale=EPS * EPS)
+        factor = shared.tile([P, 1], F32, name="factor", offset=FACTOR_AT, align_bytes=64)
+        nc.scalar.activation(factor[:], one[:], ACT.Copy, scale=-2.0 / 3.0)
         ceiling = sb.tile([P, 1], F32, name="ceiling")
         nc.scalar.activation(ceiling[:], eps[:], ACT.Copy, scale=-2.0 / 3.0)
         identity = sb.tile([P, P], F32, name="identity")
         make_identity(nc, identity[:])
+        x_scale = sb.tile([P, S], U8, name="x_scale", align_bytes=64)
+        nc.gpsimd.memset(x_scale[:].bitcast(I32), 0)
 
         def move_norms(b, picked_norms):
             member_norms = sb.tile([P, D], F32, name="member_norms%d" % b, align_bytes=64)
             nc.sync.dma_start(member_norms[:], picked_norms[P - 1 : P, :].rearrange("o (g d) -> o g d", d=D))
             return member_norms
 
-        first_norms = sb.tile([P, D * P], F32, name="first_norms", align_bytes=64)
-        nc.vector.tensor_scalar(
-            first_norms[:], norm_table[:].indirect(offsets[:, 0:32]), -2.0 / 3.0, -EPS / 1.5, ALU.mult, ALU.add
-        )
-        shift = [move_norms(0, first_norms)]
+        def gather_norms(b, picked_norms):
+            nc.scalar.activation(
+                picked_norms[:],
+                norm_table[:].indirect(offsets[:, 32 * b : 32 * (b + 1)]),
+                ACT.Copy,
+                scale=-2.0 / 3.0,
+                bias=-EPS / 1.5,
+            )
+            return move_norms(b, picked_norms)
+
+        shift = [gather_norms(0, sb.tile([P, D * P], F32, name="first_norms", align_bytes=64))]
 
         picked_scales = sb.tile([P, S], U8, name="picked_scales", tag="picked_scales", align_bytes=64)
         nc.vector.tensor_copy(picked_scales[:], scale_table[:].indirect(offsets[:]))
-        bag_raw = sb.tile([P, PACK, N], F32, name="bag_raw", tag="scale_table", align_bytes=64)
-        nc.sync.dma_start(bag_raw[:], bag.rearrange("(p j) m -> p j m", j=PACK))
+        by_member = sb.tile([P, S], U8, name="by_member", align_bytes=64)
+        nc.vector.tensor_copy(
+            by_member[:].rearrange("p (b d g) -> p b d g", b=BLOCKS, d=D),
+            picked_scales[:].rearrange("p (b g d) -> p b d g", b=BLOCKS, d=D),
+        )
+        for q in range(4):
+            rows = slice(P - SCALE_ROWS + 4 * q, P - SCALE_ROWS + 4 * q + 4)
+            nc.sync.dma_start(x_scale[32 * q : 32 * q + 4, :].bitcast(I32), by_member[rows, :].bitcast(I32))
 
-        def deal_scales(b, tag):
-            by_member = sb.tile([P, D, P], U8, name="x_scale%d" % b, tag=tag, align_bytes=64)
-            nc.vector.tensor_copy(
-                by_member[:], picked_scales[:, 512 * b : 512 * (b + 1)].rearrange("p (g d) -> p d g", d=D)
-            )
-            return by_member
-
-        x_scale = [deal_scales(0, "x_scale0")]
-
-        h_bf = sb.tile([P, PACK, P, PACK], BF16, name="h_bf", tag="h_bf", align_bytes=64)
+        h_bf = shared.tile([P, PACK, P, PACK], BF16, name="h_bf", offset=0, align_bytes=64)
         for part, (lo, hi) in enumerate(H_PARTS):
             nc.scalar.copy(
-                h_bf[:, :, lo:hi, :].rearrange("p r m j -> p m r j"),
-                h_raw[part][:].rearrange("p j (m r) -> p m r j", r=PACK),
+                h_bf[:, :, lo:hi, :].rearrange("p r m j -> p m j r"),
+                h_raw[part][:].rearrange("p j (m r) -> p m j r", r=PACK),
             )
-        h_codes = sb.tile([P, V], U32, name="h_codes", align_bytes=64)
+        own_spread = ps.tile([P, PACK, P], F32, name="own_spread", tag="bank0")
+        for r in range(PACK):
+            nc.tensor.transpose(own_spread[:, r, :], own_cols[:, r : r + 1].to_broadcast([P, P]), identity[:])
+        own_rows = sb.tile([P, PACK, P], F32, name="own_rows", tag="h_raw1", align_bytes=64)
+        nc.scalar.activation(own_rows[:], own_spread[:], ACT.Copy, scale=factor[:])
+        turned = []
+        for b in range(BLOCKS):
+            bank = ps.tile([P, PACK, P], F32, name="turned%d" % b, tag="bank%d" % (6 + b))
+            for r in range(PACK):
+                nc.tensor.matmul(
+                    bank[:, r, :], own_rows[:, r, :], identity[:], start=(r == 0), stop=False, is_transpose=True
+                )
+            turned.append(bank)
+
+        h_codes = sb.tile([P, V], U32, name="h_codes", tag="picked_scales", align_bytes=64)
         h_scale = sb.tile([P, V], U8, name="h_scale", align_bytes=64)
         nc.vector.quantize_mx(
             out=h_codes[:].bitcast(FP8X4),
@@ -117,14 +136,12 @@ def tile_picked_yrwmd_dist_p_kernel(
 
         x_codes = []
         for b in range(BLOCKS):
-            codes = sb.tile([P, D, P], U32, name="x_codes%d" % b, tag=("x_codes0", "h_bf")[b], align_bytes=64)
+            codes = shared.tile([P, D, P], U32, name="x_codes%d" % b, offset=4 * D * P * b, align_bytes=64)
             nc.vector.tensor_copy(
                 codes[:].rearrange("p d g -> p g d"),
                 word_table[:].indirect(offsets[:, 32 * b : 32 * (b + 1)]),
             )
             x_codes.append(codes)
-
-        x_scale.append(deal_scales(1, "word_table"))
 
         idf_squared = sb.tile([P, PACK], F32, name="idf_squared", tag="idf_squared", align_bytes=64)
         nc.gpsimd.tensor_tensor(idf_squared[:], idf_cols[:], idf_cols[:], ALU.mult)
@@ -135,18 +152,11 @@ def tile_picked_yrwmd_dist_p_kernel(
         idf_size = sb.tile([P, PACK], F32, name="idf_size")
         nc.gpsimd.tensor_tensor(idf_size[:], idf_cols[:], idf_sign[:], ALU.mult)
 
-        own_spread = ps.tile([P, PACK, P], F32, name="own_spread", tag="bank5")
-        for r in range(PACK):
-            nc.tensor.transpose(own_spread[:, r, :], own_cols[:, r : r + 1].to_broadcast([P, P]), identity[:])
-        own_rows = sb.tile([P, PACK, P], F32, name="own_rows")
-        nc.scalar.activation(own_rows[:], own_spread[:], ACT.Copy, scale=-2.0 / 3.0)
-        second_norms = sb.tile([P, D * P], F32, name="second_norms", tag="own_cols", align_bytes=64)
-        nc.scalar.activation(
-            second_norms[:], norm_table[:].indirect(offsets[:, 32:64]), ACT.Copy, scale=-2.0 / 3.0, bias=-EPS / 1.5
+        shift.append(
+            gather_norms(1, shared.tile([P, D * P], F32, name="second_norms", offset=FACTOR_AT, align_bytes=64))
         )
-        shift.append(move_norms(1, second_norms))
 
-        bag_bf = sb.tile([P, N, PACK], BF16, name="bag_bf", tag="picked_scales", align_bytes=64)
+        bag_bf = sb.tile([P, N, PACK], BF16, name="bag_bf", tag="word_table", align_bytes=64)
         for quarter in range(4):
             cols = slice(64 * quarter, 64 * (quarter + 1))
             nc.gpsimd.tensor_tensor(
@@ -156,16 +166,6 @@ def tile_picked_yrwmd_dist_p_kernel(
                 ALU.mult,
             )
 
-        turned = []
-        for b in range(BLOCKS):
-            bank = ps.tile([P, PACK, P], F32, name="turned%d" % b, tag="bank%d" % (6 + b))
-            for r in range(PACK):
-                nc.tensor.matmul(
-                    bank[:, r, :], own_rows[:, r, :], identity[:], start=(r == 0), stop=False, is_transpose=True
-                )
-            turned.append(bank)
-
-        best = []
         for b in range(BLOCKS):
             dots = []
             for d in range(D):
@@ -173,7 +173,7 @@ def tile_picked_yrwmd_dist_p_kernel(
                 nc.tensor.matmul_mx(
                     out=acc[:],
                     lhsT=x_codes[b][:, d, :].bitcast(FP8X4),
-                    lhsT_scale=x_scale[b][:, d, :],
+                    lhsT_scale=x_scale[:, P * (D * b + d) : P * (D * b + d + 1)],
                     rhs=h_codes[:].bitcast(FP8X4),
                     rhs_scale=h_scale[:],
                     start=True,
@@ -214,12 +214,9 @@ def tile_picked_yrwmd_dist_p_kernel(
                     ALU.max,
                 )
                 slots.extend(last[:, i, :] for i in range(hi - lo))
-            best.append(slots)
-
-        for b in range(BLOCKS):
             for r in range(PACK):
                 nc.tensor.matmul(
-                    turned[b][:, r, :], best[b][r], identity[:], start=False, stop=(r == PACK - 1), is_transpose=True
+                    turned[b][:, r, :], slots[r], identity[:], start=False, stop=(r == PACK - 1), is_transpose=True
                 )
 
         bag_codes = sb.tile([P, N], U32, name="bag_codes", tag="run1_2_1", align_bytes=64)
@@ -288,7 +285,7 @@ def tile_picked_yrwmd_dist_p_kernel(
                 stop=True,
             )
 
-        sums = ps.tile([P, N // P, P], F32, name="sums_first", tag="bank2")
+        sums = ps.tile([P, N // P, P], F32, name="sums_first", tag="bank4")
         for a in range(N // P):
             weigh(sums[:, a, :], a, 0)
         result = sb.tile([P, N // P, P], F32, name="result_first")
@@ -297,7 +294,7 @@ def tile_picked_yrwmd_dist_p_kernel(
 
         upper = ps.tile([P, P], F32, name="sums_upper", tag="bank3")
         weigh(upper[:], 0, 1)
-        lower = ps.tile([P, P], F32, name="sums_lower", tag="bank4")
+        lower = ps.tile([P, P], F32, name="sums_lower", tag="bank5")
         weigh(lower[:], 1, 1)
         upper_result = sb.tile([P, P], F32, name="upper_result")
         nc.vector.tensor_copy(upper_result[:], upper[:])

@@ -13,7 +13,7 @@ H_PARTS = ((0, 64), (64, 128))
 EPS = 0.01
 SCALE_ROWS = 16
 FACTOR_AT = 2 * PACK * V
-DOT_BANKS = ((0, 1, 2, 3), (0, 1, 2, 1))
+DOT_BANKS = ((0, 1, 2, 3), (4, 5, 0, 1))
 
 F32 = mybir.dt.float32
 BF16 = mybir.dt.bfloat16
@@ -285,7 +285,7 @@ def tile_picked_yrwmd_dist_p_kernel(
                 stop=True,
             )
 
-        sums = ps.tile([P, N // P, P], F32, name="sums_first", tag="bank4")
+        sums = ps.tile([P, N // P, P], F32, name="sums_first", tag="bank2")
         for a in range(N // P):
             weigh(sums[:, a, :], a, 0)
         result = sb.tile([P, N // P, P], F32, name="result_first")
@@ -294,7 +294,7 @@ def tile_picked_yrwmd_dist_p_kernel(
 
         upper = ps.tile([P, P], F32, name="sums_upper", tag="bank3")
         weigh(upper[:], 0, 1)
-        lower = ps.tile([P, P], F32, name="sums_lower", tag="bank5")
+        lower = ps.tile([P, P], F32, name="sums_lower", tag="bank4")
         weigh(lower[:], 1, 1)
         upper_result = sb.tile([P, P], F32, name="upper_result")
         nc.vector.tensor_copy(upper_result[:], upper[:])

@@ -9,10 +9,11 @@ PACK = 4
 G = S // D
 BLOCKS = G // P
 HALF = V // 2
-H_PARTS = ((0, 64), (64, 128))
 EPS = 0.01
 SCALE_ROWS = 16
-FACTOR_AT = 2 * PACK * V
+ROUNDED_AT = 64
+PICKED_AT = ROUNDED_AT + 2 * PACK * V
+SCALAR_SLOTS = 3
 DOT_BANKS = ((0, 1, 2, 3), (4, 5, 0, 1))
 
 F32 = mybir.dt.float32
@@ -47,12 +48,8 @@ def tile_picked_yrwmd_dist_p_kernel(
         nc.sync.dma_start(scale_table[P - SCALE_ROWS : P, :].bitcast(I32), x_scales[0].bitcast(I32))
         own_cols = sb.tile([P, PACK], F32, name="own_cols")
         nc.sync.dma_start(own_cols[:], own.rearrange("(p j) o -> p (j o)", j=PACK))
-        h_rows = hT.rearrange("(p j) t -> p j t", j=PACK)
-        h_raw = []
-        for part in range(2):
-            raw = sb.tile([P, PACK, HALF], F32, name="h_raw%d" % part, tag="h_raw%d" % part, align_bytes=64)
-            nc.sync.dma_start(raw[:], h_rows[:, :, HALF * part : HALF * (part + 1)])
-            h_raw.append(raw)
+        h_raw = sb.tile([P, PACK, V], F32, name="h_raw", tag="h_raw", align_bytes=64)
+        nc.sync.dma_start(h_raw[:], hT.rearrange("(p j) t -> p j t", j=PACK))
         word_table = sb.tile([P, T], U32, name="word_table", tag="word_table", align_bytes=64)
         nc.sync.dma_start(
             word_table[:].bitcast(I32),
@@ -69,8 +66,8 @@ def tile_picked_yrwmd_dist_p_kernel(
         nc.vector.memset(norm_table[0 : P - 1, :], 0.0)
         eps = sb.tile([P, 1], F32, name="eps")
         nc.scalar.activation(eps[:], one[:], ACT.Sqrt, scale=EPS * EPS)
-        factor = shared.tile([P, 1], F32, name="factor", offset=FACTOR_AT, align_bytes=64)
-        nc.scalar.activation(factor[:], one[:], ACT.Copy, scale=-2.0 / 3.0)
+        factor = shared.tile([P, 32], F32, name="factor", offset=0, align_bytes=64)
+        nc.scalar.activation(factor[:, 0:1], one[:], ACT.Copy, scale=-2.0 / 3.0)
         ceiling = sb.tile([P, 1], F32, name="ceiling")
         nc.scalar.activation(ceiling[:], eps[:], ACT.Copy, scale=-2.0 / 3.0)
         identity = sb.tile([P, P], F32, name="identity")
@@ -95,7 +92,7 @@ def tile_picked_yrwmd_dist_p_kernel(
 
         shift = [gather_norms(0, sb.tile([P, D * P], F32, name="first_norms", align_bytes=64))]
 
-        picked_scales = sb.tile([P, S], U8, name="picked_scales", tag="picked_scales", align_bytes=64)
+        picked_scales = shared.tile([P, S], U8, name="picked_scales", offset=PICKED_AT + S // 2, align_bytes=64)
         nc.vector.tensor_copy(picked_scales[:], scale_table[:].indirect(offsets[:]))
         by_member = sb.tile([P, S], U8, name="by_member", align_bytes=64)
         nc.vector.tensor_copy(
@@ -106,17 +103,11 @@ def tile_picked_yrwmd_dist_p_kernel(
             rows = slice(P - SCALE_ROWS + 4 * q, P - SCALE_ROWS + 4 * q + 4)
             nc.sync.dma_start(x_scale[32 * q : 32 * q + 4, :].bitcast(I32), by_member[rows, :].bitcast(I32))
 
-        h_bf = shared.tile([P, PACK, P, PACK], BF16, name="h_bf", offset=0, align_bytes=64)
-        for part, (lo, hi) in enumerate(H_PARTS):
-            nc.scalar.copy(
-                h_bf[:, :, lo:hi, :].rearrange("p r m j -> p m j r"),
-                h_raw[part][:].rearrange("p j (m r) -> p m j r", r=PACK),
-            )
         own_spread = ps.tile([P, PACK, P], F32, name="own_spread", tag="bank0")
         for r in range(PACK):
             nc.tensor.transpose(own_spread[:, r, :], own_cols[:, r : r + 1].to_broadcast([P, P]), identity[:])
-        own_rows = sb.tile([P, PACK, P], F32, name="own_rows", tag="h_raw1", align_bytes=64)
-        nc.scalar.activation(own_rows[:], own_spread[:], ACT.Copy, scale=factor[:])
+        own_rows = sb.tile([P, PACK, P], F32, name="own_rows", align_bytes=64)
+        nc.scalar.activation(own_rows[:], own_spread[:], ACT.Copy, scale=factor[:, 0:1])
         turned = []
         for b in range(BLOCKS):
             bank = ps.tile([P, PACK, P], F32, name="turned%d" % b, tag="bank%d" % (6 + b))
@@ -126,17 +117,28 @@ def tile_picked_yrwmd_dist_p_kernel(
                 )
             turned.append(bank)
 
-        h_codes = sb.tile([P, V], U32, name="h_codes", tag="picked_scales", align_bytes=64)
+        h_bf = shared.tile([P, SCALAR_SLOTS, P, PACK], BF16, name="h_bf", offset=ROUNDED_AT, align_bytes=64)
+        h_bf_last = shared.tile([P, P, PACK], BF16, name="h_bf_last", offset=PICKED_AT, align_bytes=64)
+        by_slot = h_raw[:].rearrange("p j (m r) -> p m j r", r=PACK)
+        nc.scalar.copy(h_bf[:].rearrange("p r m j -> p m j r"), by_slot[:, :, :, 0:SCALAR_SLOTS])
+        nc.vector.tensor_copy(h_bf_last[:], by_slot[:, :, :, SCALAR_SLOTS])
+        h_codes = shared.tile([P, V], U32, name="h_codes", offset=PICKED_AT + S, align_bytes=64)
         h_scale = sb.tile([P, V], U8, name="h_scale", align_bytes=64)
+        split = SCALAR_SLOTS * P
         nc.vector.quantize_mx(
-            out=h_codes[:].bitcast(FP8X4),
-            scales=h_scale[:],
+            out=h_codes[:, split:V].bitcast(FP8X4),
+            scales=h_scale[:, split:V],
+            in_=h_bf_last[:].rearrange("p m j -> p (m j)"),
+        )
+        nc.vector.quantize_mx(
+            out=h_codes[:, 0:split].bitcast(FP8X4),
+            scales=h_scale[:, 0:split],
             in_=h_bf[:].rearrange("p r m j -> p (r m j)"),
         )
 
         x_codes = []
         for b in range(BLOCKS):
-            codes = shared.tile([P, D, P], U32, name="x_codes%d" % b, offset=4 * D * P * b, align_bytes=64)
+            codes = shared.tile([P, D, P], U32, name="x_codes%d" % b, offset=ROUNDED_AT + 4 * D * P * b, align_bytes=64)
             nc.vector.tensor_copy(
                 codes[:].rearrange("p d g -> p g d"),
                 word_table[:].indirect(offsets[:, 32 * b : 32 * (b + 1)]),
@@ -153,7 +155,7 @@ def tile_picked_yrwmd_dist_p_kernel(
         nc.gpsimd.tensor_tensor(idf_size[:], idf_cols[:], idf_sign[:], ALU.mult)
 
         shift.append(
-            gather_norms(1, shared.tile([P, D * P], F32, name="second_norms", offset=FACTOR_AT, align_bytes=64))
+            gather_norms(1, sb.tile([P, D * P], F32, name="second_norms", tag="h_raw", align_bytes=64))
         )
 
         bag_bf = sb.tile([P, N, PACK], BF16, name="bag_bf", tag="word_table", align_bytes=64)

@@ -125,25 +125,27 @@ def tile_picked_yrwmd_dist_p_kernel(
         h_codes = shared.tile([P, V], U32, name="h_codes", offset=PICKED_AT + S, align_bytes=64)
         h_scale = sb.tile([P, V], U8, name="h_scale", align_bytes=64)
         split = SCALAR_SLOTS * P
+
+        def gather_words(b, offset):
+            codes = shared.tile([P, D, P], U32, name="x_codes%d" % b, offset=offset, align_bytes=64)
+            nc.vector.tensor_copy(
+                codes[:].rearrange("p d g -> p g d"),
+                word_table[:].indirect(offsets[:, 32 * b : 32 * (b + 1)]),
+            )
+            return codes
+
         nc.vector.quantize_mx(
             out=h_codes[:, split:V].bitcast(FP8X4),
             scales=h_scale[:, split:V],
             in_=h_bf_last[:].rearrange("p m j -> p (m j)"),
         )
+        x_codes = [gather_words(0, PICKED_AT - S)]
         nc.vector.quantize_mx(
             out=h_codes[:, 0:split].bitcast(FP8X4),
             scales=h_scale[:, 0:split],
             in_=h_bf[:].rearrange("p r m j -> p (r m j)"),
         )
-
-        x_codes = []
-        for b in range(BLOCKS):
-            codes = shared.tile([P, D, P], U32, name="x_codes%d" % b, offset=ROUNDED_AT + 4 * D * P * b, align_bytes=64)
-            nc.vector.tensor_copy(
-                codes[:].rearrange("p d g -> p g d"),
-                word_table[:].indirect(offsets[:, 32 * b : 32 * (b + 1)]),
-            )
-            x_codes.append(codes)
+        x_codes.append(gather_words(1, ROUNDED_AT))
 
         idf_squared = sb.tile([P, PACK], F32, name="idf_squared", tag="idf_squared", align_bytes=64)
         nc.gpsimd.tensor_tensor(idf_squared[:], idf_cols[:], idf_cols[:], ALU.mult)
@@ -159,14 +161,12 @@ def tile_picked_yrwmd_dist_p_kernel(
         )
 
         bag_bf = sb.tile([P, N, PACK], BF16, name="bag_bf", tag="word_table", align_bytes=64)
-        for quarter in range(4):
-            cols = slice(64 * quarter, 64 * (quarter + 1))
-            nc.gpsimd.tensor_tensor(
-                bag_bf[:, cols, :],
-                bag_raw[:, :, cols].rearrange("p j m -> p m j"),
-                idf_sign[:].unsqueeze(1).to_broadcast([P, 64, PACK]),
-                ALU.mult,
-            )
+        nc.gpsimd.tensor_tensor(
+            bag_bf[:],
+            bag_raw[:].rearrange("p j m -> p m j"),
+            idf_sign[:].unsqueeze(1).to_broadcast([P, N, PACK]),
+            ALU.mult,
+        )
 
         for b in range(BLOCKS):
             dots = []

@@ -11,8 +11,11 @@ BLOCKS = G // P
 HALF = V // 2
 EPS = 0.01
 SCALE_ROWS = 16
+CLEARED = 3 * T // 4
 ROUNDED_AT = 64
 PICKED_AT = ROUNDED_AT + 2 * PACK * V
+WORDS_AT = PICKED_AT + S + 4 * V
+SIGNS_AT = WORDS_AT + 2 * PACK * N
 SCALAR_SLOTS = 3
 DOT_BANKS = ((0, 1, 2, 3), (4, 5, 0, 1))
 
@@ -50,7 +53,7 @@ def tile_picked_yrwmd_dist_p_kernel(
         nc.sync.dma_start(own_cols[:], own.rearrange("(p j) o -> p (j o)", j=PACK))
         h_raw = sb.tile([P, PACK, V], F32, name="h_raw", tag="h_raw", align_bytes=64)
         nc.sync.dma_start(h_raw[:], hT.rearrange("(p j) t -> p j t", j=PACK))
-        word_table = sb.tile([P, T], U32, name="word_table", tag="word_table", align_bytes=64)
+        word_table = shared.tile([P, T], U32, name="word_table", offset=WORDS_AT, align_bytes=64)
         nc.sync.dma_start(
             word_table[:].bitcast(I32),
             x_words[0].rearrange("p c r -> p (c r)").bitcast(I32),
@@ -63,7 +66,9 @@ def tile_picked_yrwmd_dist_p_kernel(
         one = sb.tile([P, 1], F32, name="one")
         nc.vector.memset(one[:], 1.0)
         nc.gpsimd.memset(scale_table[0 : P - SCALE_ROWS, :].bitcast(I32), 0)
-        nc.vector.memset(norm_table[0 : P - 1, :], 0.0)
+        nc.vector.memset(norm_table[0 : P - 1, 0 : CLEARED - 1], 0.0)
+        nc.vector.memset(norm_table[0 : P - 1, CLEARED - 1 : CLEARED], 0.0)
+        nc.gpsimd.memset(norm_table[0 : P - 1, CLEARED:T], 0.0)
         eps = sb.tile([P, 1], F32, name="eps")
         nc.scalar.activation(eps[:], one[:], ACT.Sqrt, scale=EPS * EPS)
         factor = shared.tile([P, 32], F32, name="factor", offset=0, align_bytes=64)
@@ -76,7 +81,8 @@ def tile_picked_yrwmd_dist_p_kernel(
         nc.gpsimd.memset(x_scale[:].bitcast(I32), 0)
 
         def move_norms(b, picked_norms):
-            member_norms = sb.tile([P, D], F32, name="member_norms%d" % b, align_bytes=64)
+            name = "member_norms%d" % b
+            member_norms = sb.tile([P, D], F32, name=name, tag=name, align_bytes=64)
             nc.sync.dma_start(member_norms[:], picked_norms[P - 1 : P, :].rearrange("o (g d) -> o g d", d=D))
             return member_norms
 
@@ -147,26 +153,27 @@ def tile_picked_yrwmd_dist_p_kernel(
         )
         x_codes.append(gather_words(1, ROUNDED_AT))
 
-        idf_squared = sb.tile([P, PACK], F32, name="idf_squared", tag="idf_squared", align_bytes=64)
-        nc.gpsimd.tensor_tensor(idf_squared[:], idf_cols[:], idf_cols[:], ALU.mult)
-        idf_positive = sb.tile([P, PACK], F32, name="idf_positive")
+        idf_positive = shared.tile([P, PACK], F32, name="idf_positive", offset=SIGNS_AT, align_bytes=64)
         nc.gpsimd.tensor_scalar(idf_positive[:], idf_cols[:], 0.0, None, ALU.is_ge)
         idf_sign = sb.tile([P, PACK], F32, name="idf_sign")
         nc.gpsimd.tensor_scalar(idf_sign[:], idf_positive[:], 2.0, -1.0, ALU.mult, ALU.add)
-        idf_size = sb.tile([P, PACK], F32, name="idf_size")
-        nc.gpsimd.tensor_tensor(idf_size[:], idf_cols[:], idf_sign[:], ALU.mult)
 
         shift.append(
             gather_norms(1, sb.tile([P, D * P], F32, name="second_norms", tag="h_raw", align_bytes=64))
         )
 
-        bag_bf = sb.tile([P, N, PACK], BF16, name="bag_bf", tag="word_table", align_bytes=64)
+        bag_bf = shared.tile([P, N, PACK], BF16, name="bag_bf", offset=WORDS_AT, align_bytes=64)
         nc.gpsimd.tensor_tensor(
             bag_bf[:],
             bag_raw[:].rearrange("p j m -> p m j"),
             idf_sign[:].unsqueeze(1).to_broadcast([P, N, PACK]),
             ALU.mult,
         )
+
+        idf_size = sb.tile([P, PACK], F32, name="idf_size")
+        nc.gpsimd.tensor_tensor(idf_size[:], idf_cols[:], idf_sign[:], ALU.mult)
+        idf_squared = shared.tile([P, PACK], F32, name="idf_squared", offset=SIGNS_AT + 64, align_bytes=64)
+        nc.gpsimd.tensor_tensor(idf_squared[:], idf_cols[:], idf_cols[:], ALU.mult)
 
         for b in range(BLOCKS):
             dots = []
@@ -221,6 +228,33 @@ def tile_picked_yrwmd_dist_p_kernel(
                     turned[b][:, r, :], slots[r], identity[:], start=False, stop=(r == PACK - 1), is_transpose=True
                 )
 
+        z_bf = [sb.tile([P, P, PACK], BF16, name="z_bf%d" % b, align_bytes=64) for b in range(BLOCKS)]
+
+        def root_without_vector(b, docs):
+            clipped = sb.tile([P, 64, PACK], F32, name="clipped_early", align_bytes=64)
+            near = sb.tile([P, 64, PACK], F32, name="near", align_bytes=64)
+            nc.scalar.activation(
+                clipped[:], turned[b][:, :, docs].rearrange("p r g -> p g r"), ACT.Relu, scale=-1.5, bias=-EPS
+            )
+            nc.scalar.activation(near[:], clipped[:], ACT.Sqrt, bias=eps[:])
+            nc.gpsimd.tensor_tensor(
+                z_bf[b][:, docs, :], near[:], idf_size[:].unsqueeze(1).to_broadcast([P, 64, PACK]), ALU.mult
+            )
+
+        def root_with_vector(b, docs, tag):
+            clipped = sb.tile([P, 64, PACK], F32, name="clipped%d_%d" % (b, docs.start), tag=tag, align_bytes=64)
+            nc.vector.scalar_tensor_tensor(
+                clipped[:],
+                turned[b][:, :, docs].rearrange("p r g -> p g r"),
+                ceiling[:],
+                idf_squared[:].unsqueeze(1).to_broadcast([P, 64, PACK]),
+                ALU.min,
+                ALU.mult,
+            )
+            nc.scalar.activation(z_bf[b][:, docs, :], clipped[:], ACT.Sqrt, scale=-1.5)
+
+        root_without_vector(0, slice(0, 64))
+        root_with_vector(0, slice(64, P), "member_norms1")
         bag_codes = sb.tile([P, N], U32, name="bag_codes", tag="run1_2_1", align_bytes=64)
         bag_scale = sb.tile([P, N], U8, name="bag_scale", align_bytes=64)
         nc.vector.quantize_mx(
@@ -229,45 +263,15 @@ def tile_picked_yrwmd_dist_p_kernel(
             in_=bag_bf[:].rearrange("p m j -> p (m j)"),
         )
 
-        z_bf = []
-        for b in range(BLOCKS):
-            clipped = sb.tile([P, P, PACK], F32, name="clipped%d" % b, align_bytes=64)
-            rounded = sb.tile([P, P, PACK], BF16, name="z_bf%d" % b, align_bytes=64)
-            for half in range(2):
-                docs = slice(64 * half, 64 * (half + 1))
-                if b == 0:
-                    near = sb.tile([P, 64, PACK], F32, name="near%d" % half, align_bytes=64)
-                    nc.scalar.activation(
-                        clipped[:, docs, :],
-                        turned[b][:, :, docs].rearrange("p r g -> p g r"),
-                        ACT.Relu,
-                        scale=-1.5,
-                        bias=-EPS,
-                    )
-                    nc.scalar.activation(near[:], clipped[:, docs, :], ACT.Sqrt, bias=eps[:])
-                    nc.gpsimd.tensor_tensor(
-                        rounded[:, docs, :],
-                        near[:],
-                        idf_size[:].unsqueeze(1).to_broadcast([P, 64, PACK]),
-                        ALU.mult,
-                    )
-                else:
-                    nc.vector.scalar_tensor_tensor(
-                        clipped[:, docs, :],
-                        turned[b][:, :, docs].rearrange("p r g -> p g r"),
-                        ceiling[:],
-                        idf_squared[:].unsqueeze(1).to_broadcast([P, 64, PACK]),
-                        ALU.min,
-                        ALU.mult,
-                    )
-                    nc.scalar.activation(rounded[:, docs, :], clipped[:, docs, :], ACT.Sqrt, scale=-1.5)
-            z_bf.append(rounded)
+        root_with_vector(1, slice(0, 64), "clipped_upper")
+        root_with_vector(1, slice(64, P), "clipped_lower")
 
         z_mx = []
         for b in range(BLOCKS):
-            z_codes = sb.tile(
-                [P, P], U32, name="z_codes%d" % b, tag=("idf_squared", "z_codes1")[b], align_bytes=64
-            )
+            if b == 0:
+                z_codes = shared.tile([P, P], U32, name="z_codes0", offset=SIGNS_AT + 64, align_bytes=64)
+            else:
+                z_codes = sb.tile([P, P], U32, name="z_codes1", align_bytes=64)
             z_scale = sb.tile([P, P], U8, name="z_scale%d" % b, align_bytes=64)
             nc.vector.quantize_mx(
                 out=z_codes[:].bitcast(FP8X4),

@@ -12,11 +12,17 @@ HALF = V // 2
 EPS = 0.01
 SCALE_ROWS = 16
 CLEARED = 3 * T // 4
-ROUNDED_AT = 64
-PICKED_AT = ROUNDED_AT + 2 * PACK * V
-WORDS_AT = PICKED_AT + S + 4 * V
+SCALAR_SLOTS = 2
+HALF_ROUNDED = PACK * V
+FIRST_PICKED_AT = 4 * PACK * N - 64
+SECOND_PICKED_AT = FIRST_PICKED_AT + D * P
+IDF_AT = SECOND_PICKED_AT
+VECTOR_ROUNDED_AT = IDF_AT + 64
+SCALAR_ROUNDED_AT = VECTOR_ROUNDED_AT + HALF_ROUNDED
+FACTOR_AT = SCALAR_ROUNDED_AT + HALF_ROUNDED - 64
+CODES_AT = SCALAR_ROUNDED_AT - HALF_ROUNDED // 2
+WORDS_AT = CODES_AT + 4 * S
 SIGNS_AT = WORDS_AT + 2 * PACK * N
-SCALAR_SLOTS = 3
 DOT_BANKS = ((0, 1, 2, 3), (4, 5, 0, 1))
 
 F32 = mybir.dt.float32
@@ -58,10 +64,6 @@ def tile_picked_yrwmd_dist_p_kernel(
             word_table[:].bitcast(I32),
             x_words[0].rearrange("p c r -> p (c r)").bitcast(I32),
         )
-        bag_raw = sb.tile([P, PACK, N], F32, name="bag_raw", align_bytes=64)
-        nc.sync.dma_start(bag_raw[:], bag.rearrange("(p j) m -> p j m", j=PACK))
-        idf_cols = sb.tile([P, PACK], F32, name="idf_cols")
-        nc.sync.dma_start(idf_cols[:], idf.rearrange("(p j) o -> p (j o)", j=PACK))
 
         one = sb.tile([P, 1], F32, name="one")
         nc.vector.memset(one[:], 1.0)
@@ -71,14 +73,17 @@ def tile_picked_yrwmd_dist_p_kernel(
         nc.gpsimd.memset(norm_table[0 : P - 1, CLEARED:T], 0.0)
         eps = sb.tile([P, 1], F32, name="eps")
         nc.scalar.activation(eps[:], one[:], ACT.Sqrt, scale=EPS * EPS)
-        factor = shared.tile([P, 32], F32, name="factor", offset=0, align_bytes=64)
+        factor = shared.tile([P, 32], F32, name="factor", offset=FACTOR_AT, align_bytes=64)
         nc.scalar.activation(factor[:, 0:1], one[:], ACT.Copy, scale=-2.0 / 3.0)
         ceiling = sb.tile([P, 1], F32, name="ceiling")
         nc.scalar.activation(ceiling[:], eps[:], ACT.Copy, scale=-2.0 / 3.0)
         identity = sb.tile([P, P], F32, name="identity")
         make_identity(nc, identity[:])
-        x_scale = sb.tile([P, S], U8, name="x_scale", align_bytes=64)
-        nc.gpsimd.memset(x_scale[:].bitcast(I32), 0)
+        x_scale = []
+        for b in range(BLOCKS):
+            plane = sb.tile([P, D * P], U8, name="x_scale%d" % b, align_bytes=64)
+            nc.gpsimd.memset(plane[:].bitcast(I32), 0)
+            x_scale.append(plane)
 
         def move_norms(b, picked_norms):
             name = "member_norms%d" % b
@@ -98,16 +103,26 @@ def tile_picked_yrwmd_dist_p_kernel(
 
         shift = [gather_norms(0, sb.tile([P, D * P], F32, name="first_norms", align_bytes=64))]
 
-        picked_scales = shared.tile([P, S], U8, name="picked_scales", offset=PICKED_AT + S // 2, align_bytes=64)
-        nc.vector.tensor_copy(picked_scales[:], scale_table[:].indirect(offsets[:]))
-        by_member = sb.tile([P, S], U8, name="by_member", align_bytes=64)
-        nc.vector.tensor_copy(
-            by_member[:].rearrange("p (b d g) -> p b d g", b=BLOCKS, d=D),
-            picked_scales[:].rearrange("p (b g d) -> p b d g", b=BLOCKS, d=D),
-        )
-        for q in range(4):
-            rows = slice(P - SCALE_ROWS + 4 * q, P - SCALE_ROWS + 4 * q + 4)
-            nc.sync.dma_start(x_scale[32 * q : 32 * q + 4, :].bitcast(I32), by_member[rows, :].bitcast(I32))
+        picked_scales = [
+            shared.tile([P, D * P], U8, name="picked_scales%d" % b, offset=offset, align_bytes=64)
+            for b, offset in enumerate((FIRST_PICKED_AT, SECOND_PICKED_AT))
+        ]
+        for b in range(BLOCKS):
+            nc.vector.tensor_copy(picked_scales[b][:], scale_table[:].indirect(offsets[:, 32 * b : 32 * (b + 1)]))
+        for b in range(BLOCKS):
+            by_member = sb.tile([P, D * P], U8, name="by_member%d" % b, align_bytes=64)
+            nc.vector.tensor_copy(
+                by_member[:].rearrange("p (d g) -> p d g", d=D),
+                picked_scales[b][:].rearrange("p (g d) -> p d g", d=D),
+            )
+            for q in range(4):
+                rows = slice(P - SCALE_ROWS + 4 * q, P - SCALE_ROWS + 4 * q + 4)
+                nc.sync.dma_start(x_scale[b][32 * q : 32 * q + 4, :].bitcast(I32), by_member[rows, :].bitcast(I32))
+            if b == 0:
+                bag_raw = shared.tile([P, PACK, N], F32, name="bag_raw", offset=0, align_bytes=64)
+                nc.sync.dma_start(bag_raw[:], bag.rearrange("(p j) m -> p j m", j=PACK))
+        idf_cols = shared.tile([P, PACK], F32, name="idf_cols", offset=IDF_AT, align_bytes=64)
+        nc.sync.dma_start(idf_cols[:], idf.rearrange("(p j) o -> p (j o)", j=PACK))
 
         own_spread = ps.tile([P, PACK, P], F32, name="own_spread", tag="bank0")
         for r in range(PACK):
@@ -123,40 +138,40 @@ def tile_picked_yrwmd_dist_p_kernel(
                 )
             turned.append(bank)
 
-        h_bf = shared.tile([P, SCALAR_SLOTS, P, PACK], BF16, name="h_bf", offset=ROUNDED_AT, align_bytes=64)
-        h_bf_last = shared.tile([P, P, PACK], BF16, name="h_bf_last", offset=PICKED_AT, align_bytes=64)
         by_slot = h_raw[:].rearrange("p j (m r) -> p m j r", r=PACK)
+        h_bf = shared.tile([P, SCALAR_SLOTS, P, PACK], BF16, name="h_bf", offset=SCALAR_ROUNDED_AT, align_bytes=64)
         nc.scalar.copy(h_bf[:].rearrange("p r m j -> p m j r"), by_slot[:, :, :, 0:SCALAR_SLOTS])
-        nc.vector.tensor_copy(h_bf_last[:], by_slot[:, :, :, SCALAR_SLOTS])
-        h_codes = shared.tile([P, V], U32, name="h_codes", offset=PICKED_AT + S, align_bytes=64)
+        h_bf_last = shared.tile(
+            [P, PACK - SCALAR_SLOTS, P, PACK], BF16, name="h_bf_last", offset=VECTOR_ROUNDED_AT, align_bytes=64
+        )
+        nc.vector.tensor_copy(h_bf_last[:].rearrange("p r m j -> p m j r"), by_slot[:, :, :, SCALAR_SLOTS:PACK])
+        h_codes = sb.tile([P, V], U32, name="h_codes", align_bytes=64)
         h_scale = sb.tile([P, V], U8, name="h_scale", align_bytes=64)
         split = SCALAR_SLOTS * P
+        for rounded, cols in ((h_bf_last, slice(split, V)), (h_bf, slice(0, split))):
+            nc.vector.quantize_mx(
+                out=h_codes[:, cols].bitcast(FP8X4),
+                scales=h_scale[:, cols],
+                in_=rounded[:].rearrange("p r m j -> p (r m j)"),
+            )
 
-        def gather_words(b, offset):
-            codes = shared.tile([P, D, P], U32, name="x_codes%d" % b, offset=offset, align_bytes=64)
+        x_codes = []
+        for b in range(BLOCKS):
+            codes = shared.tile([P, D, P], U32, name="x_codes%d" % b, offset=CODES_AT + 4 * D * P * b, align_bytes=64)
             nc.vector.tensor_copy(
                 codes[:].rearrange("p d g -> p g d"),
                 word_table[:].indirect(offsets[:, 32 * b : 32 * (b + 1)]),
             )
-            return codes
-
-        nc.vector.quantize_mx(
-            out=h_codes[:, split:V].bitcast(FP8X4),
-            scales=h_scale[:, split:V],
-            in_=h_bf_last[:].rearrange("p m j -> p (m j)"),
-        )
-        x_codes = [gather_words(0, PICKED_AT - S)]
-        nc.vector.quantize_mx(
-            out=h_codes[:, 0:split].bitcast(FP8X4),
-            scales=h_scale[:, 0:split],
-            in_=h_bf[:].rearrange("p r m j -> p (r m j)"),
-        )
-        x_codes.append(gather_words(1, ROUNDED_AT))
+            x_codes.append(codes)
 
         idf_positive = shared.tile([P, PACK], F32, name="idf_positive", offset=SIGNS_AT, align_bytes=64)
         nc.gpsimd.tensor_scalar(idf_positive[:], idf_cols[:], 0.0, None, ALU.is_ge)
         idf_sign = sb.tile([P, PACK], F32, name="idf_sign")
         nc.gpsimd.tensor_scalar(idf_sign[:], idf_positive[:], 2.0, -1.0, ALU.mult, ALU.add)
+        idf_size = sb.tile([P, PACK], F32, name="idf_size")
+        nc.gpsimd.tensor_tensor(idf_size[:], idf_cols[:], idf_sign[:], ALU.mult)
+        idf_squared = shared.tile([P, PACK], F32, name="idf_squared", offset=SIGNS_AT + 64, align_bytes=64)
+        nc.gpsimd.tensor_tensor(idf_squared[:], idf_cols[:], idf_cols[:], ALU.mult)
 
         shift.append(
             gather_norms(1, sb.tile([P, D * P], F32, name="second_norms", tag="h_raw", align_bytes=64))
@@ -170,32 +185,36 @@ def tile_picked_yrwmd_dist_p_kernel(
             ALU.mult,
         )
 
-        idf_size = sb.tile([P, PACK], F32, name="idf_size")
-        nc.gpsimd.tensor_tensor(idf_size[:], idf_cols[:], idf_sign[:], ALU.mult)
-        idf_squared = shared.tile([P, PACK], F32, name="idf_squared", offset=SIGNS_AT + 64, align_bytes=64)
-        nc.gpsimd.tensor_tensor(idf_squared[:], idf_cols[:], idf_cols[:], ALU.mult)
+        def multiply(b, d, cols, bank):
+            name = "dots%d_%d_%d" % (b, d, cols.start)
+            acc = ps.tile([P, cols.stop - cols.start], F32, name=name, tag="bank%d" % bank)
+            nc.tensor.matmul_mx(
+                out=acc[:],
+                lhsT=x_codes[b][:, d, :].bitcast(FP8X4),
+                lhsT_scale=x_scale[b][:, P * d : P * (d + 1)],
+                rhs=h_codes[:, cols].bitcast(FP8X4),
+                rhs_scale=h_scale[:, cols],
+                start=True,
+                stop=True,
+            )
+            return acc
 
+        halves = (slice(0, HALF), slice(HALF, V))
         for b in range(BLOCKS):
-            dots = []
-            for d in range(D):
-                acc = ps.tile([P, V], F32, name="dots%d_%d" % (b, d), tag="bank%d" % DOT_BANKS[b][d])
-                nc.tensor.matmul_mx(
-                    out=acc[:],
-                    lhsT=x_codes[b][:, d, :].bitcast(FP8X4),
-                    lhsT_scale=x_scale[:, P * (D * b + d) : P * (D * b + d + 1)],
-                    rhs=h_codes[:].bitcast(FP8X4),
-                    rhs_scale=h_scale[:],
-                    start=True,
-                    stop=True,
-                )
-                dots.append(acc)
+            if b == 0:
+                opening = [
+                    multiply(0, 0, halves[0], DOT_BANKS[0][0])[:],
+                    multiply(0, 0, halves[1], DOT_BANKS[1][0])[:],
+                ]
+            else:
+                whole = multiply(b, 0, slice(0, V), DOT_BANKS[b][0])
+                opening = [whole[:, cols] for cols in halves]
+            dots = [None] + [multiply(b, d, slice(0, V), DOT_BANKS[b][d]) for d in range(1, D)]
             run = []
             for half in range(2):
                 tag = "run%d_0_%d" % (b, half)
                 first = sb.tile([P, HALF], F32, name="run%d_0_%d" % (b, half), tag=tag, align_bytes=64)
-                nc.scalar.activation(
-                    first[:], dots[0][:, half * HALF : (half + 1) * HALF], ACT.Identity, bias=shift[b][:, 0:1]
-                )
+                nc.scalar.activation(first[:], opening[half], ACT.Identity, bias=shift[b][:, 0:1])
                 run.append(first)
             for d in range(1, D - 1):
                 for half in range(2):

@@ -53,7 +53,7 @@ def tile_picked_yrwmd_dist_p_kernel(
 
         norm_table = sb.tile([P, T], F32, name="norm_table", align_bytes=64)
         nc.scalar.dma_start(norm_table[P - 1 : P, :], qn[0:1, :])
-        scale_table = sb.tile([P, T], U8, name="scale_table", tag="scale_table", align_bytes=64)
+        scale_table = shared.tile([P, T], U8, name="scale_table", offset=VECTOR_ROUNDED_AT - T, align_bytes=64)
         nc.sync.dma_start(scale_table[P - SCALE_ROWS : P, :].bitcast(I32), x_scales[0].bitcast(I32))
         own_cols = sb.tile([P, PACK], F32, name="own_cols")
         nc.sync.dma_start(own_cols[:], own.rearrange("(p j) o -> p (j o)", j=PACK))
@@ -103,24 +103,22 @@ def tile_picked_yrwmd_dist_p_kernel(
 
         shift = [gather_norms(0, sb.tile([P, D * P], F32, name="first_norms", align_bytes=64))]
 
-        picked_scales = [
-            shared.tile([P, D * P], U8, name="picked_scales%d" % b, offset=offset, align_bytes=64)
-            for b, offset in enumerate((FIRST_PICKED_AT, SECOND_PICKED_AT))
-        ]
+        picked_scales = []
         for b in range(BLOCKS):
-            nc.vector.tensor_copy(picked_scales[b][:], scale_table[:].indirect(offsets[:, 32 * b : 32 * (b + 1)]))
-        for b in range(BLOCKS):
-            by_member = sb.tile([P, D * P], U8, name="by_member%d" % b, align_bytes=64)
+            by_member = sb.tile([P, D, P], U8, name="by_member%d" % b, align_bytes=64)
             nc.vector.tensor_copy(
-                by_member[:].rearrange("p (d g) -> p d g", d=D),
-                picked_scales[b][:].rearrange("p (g d) -> p d g", d=D),
+                by_member[:].rearrange("p d g -> p g d"), scale_table[:].indirect(offsets[:, 32 * b : 32 * (b + 1)])
             )
+            picked_scales.append(by_member)
+        for b in range(BLOCKS):
             for q in range(4):
                 rows = slice(P - SCALE_ROWS + 4 * q, P - SCALE_ROWS + 4 * q + 4)
-                nc.sync.dma_start(x_scale[b][32 * q : 32 * q + 4, :].bitcast(I32), by_member[rows, :].bitcast(I32))
-            if b == 0:
-                bag_raw = shared.tile([P, PACK, N], F32, name="bag_raw", offset=0, align_bytes=64)
-                nc.sync.dma_start(bag_raw[:], bag.rearrange("(p j) m -> p j m", j=PACK))
+                nc.sync.dma_start(
+                    x_scale[b][32 * q : 32 * q + 4, :].bitcast(I32),
+                    picked_scales[b][rows].rearrange("p d g -> p (d g)").bitcast(I32),
+                )
+        bag_raw = shared.tile([P, PACK, N], F32, name="bag_raw", offset=0, align_bytes=64)
+        nc.sync.dma_start(bag_raw[:], bag.rearrange("(p j) m -> p j m", j=PACK))
         idf_cols = shared.tile([P, PACK], F32, name="idf_cols", offset=IDF_AT, align_bytes=64)
         nc.sync.dma_start(idf_cols[:], idf.rearrange("(p j) o -> p (j o)", j=PACK))
 

@@ -11,18 +11,22 @@ BLOCKS = G // P
 HALF = V // 2
 EPS = 0.01
 SCALE_ROWS = 16
-CLEARED = 3 * T // 4
+CLEARED = T // 2
 SCALAR_SLOTS = 2
 HALF_ROUNDED = PACK * V
-FIRST_PICKED_AT = 4 * PACK * N - 64
-SECOND_PICKED_AT = FIRST_PICKED_AT + D * P
-IDF_AT = SECOND_PICKED_AT
-VECTOR_ROUNDED_AT = IDF_AT + 64
+VECTOR_ROUNDED_AT = 0
 SCALAR_ROUNDED_AT = VECTOR_ROUNDED_AT + HALF_ROUNDED
-FACTOR_AT = SCALAR_ROUNDED_AT + HALF_ROUNDED - 64
+SCALES_AT = SCALAR_ROUNDED_AT - T // 2
 CODES_AT = SCALAR_ROUNDED_AT - HALF_ROUNDED // 2
 WORDS_AT = CODES_AT + 4 * S
 SIGNS_AT = WORDS_AT + 2 * PACK * N
+BAG_AT = WORDS_AT + 4 * T
+OWN_AT = BAG_AT + 4 * PACK * N - 64
+IDF_AT = OWN_AT + 64
+NORMS_AT = IDF_AT + 64
+RAW_AT = NORMS_AT + 64
+SPREAD_AT = RAW_AT + 4 * D * P
+BANK = 2048
 DOT_BANKS = ((0, 1, 2, 3), (4, 5, 0, 1))
 
 F32 = mybir.dt.float32
@@ -53,11 +57,12 @@ def tile_picked_yrwmd_dist_p_kernel(
 
         norm_table = sb.tile([P, T], F32, name="norm_table", align_bytes=64)
         nc.scalar.dma_start(norm_table[P - 1 : P, :], qn[0:1, :])
-        scale_table = shared.tile([P, T], U8, name="scale_table", offset=VECTOR_ROUNDED_AT - T, align_bytes=64)
+        scale_table = shared.tile([P, T], U8, name="scale_table", offset=SCALES_AT, align_bytes=64)
         nc.sync.dma_start(scale_table[P - SCALE_ROWS : P, :].bitcast(I32), x_scales[0].bitcast(I32))
-        own_cols = sb.tile([P, PACK], F32, name="own_cols")
-        nc.sync.dma_start(own_cols[:], own.rearrange("(p j) o -> p (j o)", j=PACK))
-        h_raw = sb.tile([P, PACK, V], F32, name="h_raw", tag="h_raw", align_bytes=64)
+        own_wide = shared.tile([P, 48], F32, name="own_cols", offset=OWN_AT, align_bytes=64)
+        own_cols = own_wide[:, 0:PACK]
+        nc.sync.dma_start(own_cols, own.rearrange("(p j) o -> p (j o)", j=PACK))
+        h_raw = shared.tile([P, PACK, V], F32, name="h_raw", offset=RAW_AT, align_bytes=64)
         nc.sync.dma_start(h_raw[:], hT.rearrange("(p j) t -> p j t", j=PACK))
         word_table = shared.tile([P, T], U32, name="word_table", offset=WORDS_AT, align_bytes=64)
         nc.sync.dma_start(
@@ -66,24 +71,20 @@ def tile_picked_yrwmd_dist_p_kernel(
         )
 
         one = sb.tile([P, 1], F32, name="one")
-        nc.vector.memset(one[:], 1.0)
-        nc.gpsimd.memset(scale_table[0 : P - SCALE_ROWS, :].bitcast(I32), 0)
+        nc.gpsimd.memset(one[:], 1.0)
         nc.vector.memset(norm_table[0 : P - 1, 0 : CLEARED - 1], 0.0)
         nc.vector.memset(norm_table[0 : P - 1, CLEARED - 1 : CLEARED], 0.0)
         nc.gpsimd.memset(norm_table[0 : P - 1, CLEARED:T], 0.0)
+        nc.gpsimd.memset(scale_table[0 : P - SCALE_ROWS, :].bitcast(I32), 0)
         eps = sb.tile([P, 1], F32, name="eps")
         nc.scalar.activation(eps[:], one[:], ACT.Sqrt, scale=EPS * EPS)
-        factor = shared.tile([P, 32], F32, name="factor", offset=FACTOR_AT, align_bytes=64)
-        nc.scalar.activation(factor[:, 0:1], one[:], ACT.Copy, scale=-2.0 / 3.0)
-        ceiling = sb.tile([P, 1], F32, name="ceiling")
-        nc.scalar.activation(ceiling[:], eps[:], ACT.Copy, scale=-2.0 / 3.0)
+        planes = sb.tile([P, S], U8, name="x_scale", align_bytes=64)
+        nc.gpsimd.memset(planes[:].bitcast(I32), 0)
+        x_scale = [planes[:, b * D * P : (b + 1) * D * P] for b in range(BLOCKS)]
         identity = sb.tile([P, P], F32, name="identity")
         make_identity(nc, identity[:])
-        x_scale = []
-        for b in range(BLOCKS):
-            plane = sb.tile([P, D * P], U8, name="x_scale%d" % b, align_bytes=64)
-            nc.gpsimd.memset(plane[:].bitcast(I32), 0)
-            x_scale.append(plane)
+        ceiling = sb.tile([P, 1], F32, name="ceiling")
+        nc.gpsimd.tensor_scalar(ceiling[:], one[:], -EPS / 1.5, 0.0, ALU.mult, ALU.add)
 
         def move_norms(b, picked_norms):
             name = "member_norms%d" % b
@@ -103,38 +104,20 @@ def tile_picked_yrwmd_dist_p_kernel(
 
         shift = [gather_norms(0, sb.tile([P, D * P], F32, name="first_norms", align_bytes=64))]
 
-        picked_scales = []
-        for b in range(BLOCKS):
-            by_member = sb.tile([P, D, P], U8, name="by_member%d" % b, align_bytes=64)
-            nc.vector.tensor_copy(
-                by_member[:].rearrange("p d g -> p g d"), scale_table[:].indirect(offsets[:, 32 * b : 32 * (b + 1)])
+        picked_scales = sb.tile([P, BLOCKS, D, P], U8, name="picked_scales", align_bytes=64)
+        nc.vector.tensor_copy(
+            picked_scales[:].rearrange("p b d g -> p b g d"), scale_table[:].indirect(offsets[:])
+        )
+        for q in range(4):
+            rows = slice(P - SCALE_ROWS + 4 * q, P - SCALE_ROWS + 4 * q + 4)
+            nc.sync.dma_start(
+                planes[32 * q : 32 * q + 4, :].bitcast(I32),
+                picked_scales[rows].rearrange("p b d g -> p (b d g)").bitcast(I32),
             )
-            picked_scales.append(by_member)
-        for b in range(BLOCKS):
-            for q in range(4):
-                rows = slice(P - SCALE_ROWS + 4 * q, P - SCALE_ROWS + 4 * q + 4)
-                nc.sync.dma_start(
-                    x_scale[b][32 * q : 32 * q + 4, :].bitcast(I32),
-                    picked_scales[b][rows].rearrange("p d g -> p (d g)").bitcast(I32),
-                )
-        bag_raw = shared.tile([P, PACK, N], F32, name="bag_raw", offset=0, align_bytes=64)
+        bag_raw = shared.tile([P, PACK, N], F32, name="bag_raw", offset=BAG_AT, align_bytes=64)
         nc.sync.dma_start(bag_raw[:], bag.rearrange("(p j) m -> p j m", j=PACK))
         idf_cols = shared.tile([P, PACK], F32, name="idf_cols", offset=IDF_AT, align_bytes=64)
         nc.sync.dma_start(idf_cols[:], idf.rearrange("(p j) o -> p (j o)", j=PACK))
-
-        own_spread = ps.tile([P, PACK, P], F32, name="own_spread", tag="bank0")
-        for r in range(PACK):
-            nc.tensor.transpose(own_spread[:, r, :], own_cols[:, r : r + 1].to_broadcast([P, P]), identity[:])
-        own_rows = sb.tile([P, PACK, P], F32, name="own_rows", align_bytes=64)
-        nc.scalar.activation(own_rows[:], own_spread[:], ACT.Copy, scale=factor[:, 0:1])
-        turned = []
-        for b in range(BLOCKS):
-            bank = ps.tile([P, PACK, P], F32, name="turned%d" % b, tag="bank%d" % (6 + b))
-            for r in range(PACK):
-                nc.tensor.matmul(
-                    bank[:, r, :], own_rows[:, r, :], identity[:], start=(r == 0), stop=False, is_transpose=True
-                )
-            turned.append(bank)
 
         by_slot = h_raw[:].rearrange("p j (m r) -> p m j r", r=PACK)
         h_bf = shared.tile([P, SCALAR_SLOTS, P, PACK], BF16, name="h_bf", offset=SCALAR_ROUNDED_AT, align_bytes=64)
@@ -152,6 +135,23 @@ def tile_picked_yrwmd_dist_p_kernel(
                 scales=h_scale[:, cols],
                 in_=rounded[:].rearrange("p r m j -> p (r m j)"),
             )
+
+        spread_banks = ps.tile([P, 6, PACK, P], F32, name="own_spread", offset=0)
+        own_spread = spread_banks[:, 0]
+        for r in range(PACK):
+            nc.tensor.transpose(own_spread[:, r, :], own_cols[:, r : r + 1].to_broadcast([P, P]), identity[:])
+        own_rows = shared.tile([P, PACK, P], F32, name="own_rows", offset=SPREAD_AT, align_bytes=64)
+        nc.scalar.activation(own_rows[:], own_spread, ACT.Copy, scale=-2.0 / 3.0)
+
+        def lay_own(b, bank):
+            laid = ps.tile([P, PACK, P], F32, name="turned%d" % b, offset=BANK * (bank))
+            for r in range(PACK):
+                nc.tensor.matmul(
+                    laid[:, r, :], own_rows[:, r, :], identity[:], start=(r == 0), stop=False, is_transpose=True
+                )
+            return laid
+
+        turned = [lay_own(0, 6)]
 
         x_codes = []
         for b in range(BLOCKS):
@@ -172,7 +172,7 @@ def tile_picked_yrwmd_dist_p_kernel(
         nc.gpsimd.tensor_tensor(idf_squared[:], idf_cols[:], idf_cols[:], ALU.mult)
 
         shift.append(
-            gather_norms(1, sb.tile([P, D * P], F32, name="second_norms", tag="h_raw", align_bytes=64))
+            gather_norms(1, shared.tile([P, D * P], F32, name="second_norms", offset=NORMS_AT, align_bytes=64))
         )
 
         bag_bf = shared.tile([P, N, PACK], BF16, name="bag_bf", offset=WORDS_AT, align_bytes=64)
@@ -185,7 +185,7 @@ def tile_picked_yrwmd_dist_p_kernel(
 
         def multiply(b, d, cols, bank):
             name = "dots%d_%d_%d" % (b, d, cols.start)
-            acc = ps.tile([P, cols.stop - cols.start], F32, name=name, tag="bank%d" % bank)
+            acc = ps.tile([P, cols.stop - cols.start], F32, name=name, offset=BANK * (bank))
             nc.tensor.matmul_mx(
                 out=acc[:],
                 lhsT=x_codes[b][:, d, :].bitcast(FP8X4),
@@ -230,7 +230,10 @@ def tile_picked_yrwmd_dist_p_kernel(
                     run[half] = nxt
             slots = []
             for lo, hi in (((0, 2), (2, 4)), ((0, 2), (2, 3), (3, 4)))[b]:
-                last = sb.tile([P, hi - lo, P], F32, name="best%d_%d" % (b, lo))
+                if (b, lo) == (0, 2):
+                    last = shared.tile([P, 2, P], F32, name="best0_2", offset=NORMS_AT, align_bytes=64)
+                else:
+                    last = sb.tile([P, hi - lo, P], F32, name="best%d_%d" % (b, lo))
                 nc.vector.scalar_tensor_tensor(
                     last[:].rearrange("p r m -> p (r m)"),
                     dots[D - 1][:, lo * P : hi * P],
@@ -244,6 +247,8 @@ def tile_picked_yrwmd_dist_p_kernel(
                 nc.tensor.matmul(
                     turned[b][:, r, :], slots[r], identity[:], start=False, stop=(r == PACK - 1), is_transpose=True
                 )
+            if b == 0:
+                turned.append(lay_own(1, DOT_BANKS[0][D - 1]))
 
         z_bf = [sb.tile([P, P, PACK], BF16, name="z_bf%d" % b, align_bytes=64) for b in range(BLOCKS)]
 
@@ -308,16 +313,16 @@ def tile_picked_yrwmd_dist_p_kernel(
                 stop=True,
             )
 
-        sums = ps.tile([P, N // P, P], F32, name="sums_first", tag="bank2")
+        sums = ps.tile([P, N // P, P], F32, name="sums_first", offset=BANK * 2)
         for a in range(N // P):
             weigh(sums[:, a, :], a, 0)
         result = sb.tile([P, N // P, P], F32, name="result_first")
         nc.scalar.copy(result[:], sums[:])
         nc.sync.dma_start(out.rearrange("(a p) g -> p a g", p=P)[:, :, 0:P], result[:])
 
-        upper = ps.tile([P, P], F32, name="sums_upper", tag="bank3")
+        upper = ps.tile([P, P], F32, name="sums_upper", offset=BANK * 7)
         weigh(upper[:], 0, 1)
-        lower = ps.tile([P, P], F32, name="sums_lower", tag="bank4")
+        lower = ps.tile([P, P], F32, name="sums_lower", offset=BANK * 4)
         weigh(lower[:], 1, 1)
         upper_result = sb.tile([P, P], F32, name="upper_result")
         nc.vector.tensor_copy(upper_result[:], upper[:])

@@ -12,20 +12,16 @@ HALF = V // 2
 EPS = 0.01
 SCALE_ROWS = 16
 CLEARED = T // 2
-SCALAR_SLOTS = 2
-HALF_ROUNDED = PACK * V
-VECTOR_ROUNDED_AT = 0
-SCALAR_ROUNDED_AT = VECTOR_ROUNDED_AT + HALF_ROUNDED
-SCALES_AT = SCALAR_ROUNDED_AT - T // 2
-CODES_AT = SCALAR_ROUNDED_AT - HALF_ROUNDED // 2
+SPLIT = 3 * V // 4
+IDF_AT = 4 * PACK * N
+SCALES_AT = IDF_AT - 64
+VECTOR_ROUNDED_AT = SCALES_AT + T - 64
+SCALAR_ROUNDED_AT = VECTOR_ROUNDED_AT + 2 * PACK * SPLIT
+FACTOR_AT = SCALAR_ROUNDED_AT + 64
+CODES_AT = SCALAR_ROUNDED_AT + PACK * (V - SPLIT) - 4 * D * P
 WORDS_AT = CODES_AT + 4 * S
 SIGNS_AT = WORDS_AT + 2 * PACK * N
-BAG_AT = WORDS_AT + 4 * T
-OWN_AT = BAG_AT + 4 * PACK * N - 64
-IDF_AT = OWN_AT + 64
-NORMS_AT = IDF_AT + 64
-RAW_AT = NORMS_AT + 64
-SPREAD_AT = RAW_AT + 4 * D * P
+RAW_AT = WORDS_AT + 4 * T
 BANK = 2048
 DOT_BANKS = ((0, 1, 2, 3), (4, 5, 0, 1))
 
@@ -59,9 +55,8 @@ def tile_picked_yrwmd_dist_p_kernel(
         nc.scalar.dma_start(norm_table[P - 1 : P, :], qn[0:1, :])
         scale_table = shared.tile([P, T], U8, name="scale_table", offset=SCALES_AT, align_bytes=64)
         nc.sync.dma_start(scale_table[P - SCALE_ROWS : P, :].bitcast(I32), x_scales[0].bitcast(I32))
-        own_wide = shared.tile([P, 48], F32, name="own_cols", offset=OWN_AT, align_bytes=64)
-        own_cols = own_wide[:, 0:PACK]
-        nc.sync.dma_start(own_cols, own.rearrange("(p j) o -> p (j o)", j=PACK))
+        own_cols = sb.tile([P, PACK], F32, name="own_cols")
+        nc.sync.dma_start(own_cols[:], own.rearrange("(p j) o -> p (j o)", j=PACK))
         h_raw = shared.tile([P, PACK, V], F32, name="h_raw", offset=RAW_AT, align_bytes=64)
         nc.sync.dma_start(h_raw[:], hT.rearrange("(p j) t -> p j t", j=PACK))
         word_table = shared.tile([P, T], U32, name="word_table", offset=WORDS_AT, align_bytes=64)
@@ -74,15 +69,17 @@ def tile_picked_yrwmd_dist_p_kernel(
         nc.gpsimd.memset(one[:], 1.0)
         nc.vector.memset(norm_table[0 : P - 1, 0 : CLEARED - 1], 0.0)
         nc.vector.memset(norm_table[0 : P - 1, CLEARED - 1 : CLEARED], 0.0)
-        nc.gpsimd.memset(norm_table[0 : P - 1, CLEARED:T], 0.0)
         nc.gpsimd.memset(scale_table[0 : P - SCALE_ROWS, :].bitcast(I32), 0)
+        nc.gpsimd.memset(norm_table[0 : P - 1, CLEARED:T], 0.0)
         eps = sb.tile([P, 1], F32, name="eps")
         nc.scalar.activation(eps[:], one[:], ACT.Sqrt, scale=EPS * EPS)
-        planes = sb.tile([P, S], U8, name="x_scale", align_bytes=64)
-        nc.gpsimd.memset(planes[:].bitcast(I32), 0)
-        x_scale = [planes[:, b * D * P : (b + 1) * D * P] for b in range(BLOCKS)]
         identity = sb.tile([P, P], F32, name="identity")
         make_identity(nc, identity[:])
+        factor = shared.tile([P, 16], F32, name="factor", offset=FACTOR_AT, align_bytes=64)
+        nc.gpsimd.tensor_scalar(factor[:, 0:1], one[:], -2.0 / 3.0, 0.0, ALU.mult, ALU.add)
+        planes = sb.tile([P, S], U8, name="x_scale", align_bytes=64)
+        nc.vector.memset(planes[:].bitcast(I32), 0)
+        x_scale = [planes[:, b * D * P : (b + 1) * D * P] for b in range(BLOCKS)]
         ceiling = sb.tile([P, 1], F32, name="ceiling")
         nc.gpsimd.tensor_scalar(ceiling[:], one[:], -EPS / 1.5, 0.0, ALU.mult, ALU.add)
 
@@ -114,34 +111,17 @@ def tile_picked_yrwmd_dist_p_kernel(
                 planes[32 * q : 32 * q + 4, :].bitcast(I32),
                 picked_scales[rows].rearrange("p b d g -> p (b d g)").bitcast(I32),
             )
-        bag_raw = shared.tile([P, PACK, N], F32, name="bag_raw", offset=BAG_AT, align_bytes=64)
+        bag_raw = shared.tile([P, PACK, N], F32, name="bag_raw", offset=0, align_bytes=64)
         nc.sync.dma_start(bag_raw[:], bag.rearrange("(p j) m -> p j m", j=PACK))
         idf_cols = shared.tile([P, PACK], F32, name="idf_cols", offset=IDF_AT, align_bytes=64)
         nc.sync.dma_start(idf_cols[:], idf.rearrange("(p j) o -> p (j o)", j=PACK))
-
-        by_slot = h_raw[:].rearrange("p j (m r) -> p m j r", r=PACK)
-        h_bf = shared.tile([P, SCALAR_SLOTS, P, PACK], BF16, name="h_bf", offset=SCALAR_ROUNDED_AT, align_bytes=64)
-        nc.scalar.copy(h_bf[:].rearrange("p r m j -> p m j r"), by_slot[:, :, :, 0:SCALAR_SLOTS])
-        h_bf_last = shared.tile(
-            [P, PACK - SCALAR_SLOTS, P, PACK], BF16, name="h_bf_last", offset=VECTOR_ROUNDED_AT, align_bytes=64
-        )
-        nc.vector.tensor_copy(h_bf_last[:].rearrange("p r m j -> p m j r"), by_slot[:, :, :, SCALAR_SLOTS:PACK])
-        h_codes = sb.tile([P, V], U32, name="h_codes", align_bytes=64)
-        h_scale = sb.tile([P, V], U8, name="h_scale", align_bytes=64)
-        split = SCALAR_SLOTS * P
-        for rounded, cols in ((h_bf_last, slice(split, V)), (h_bf, slice(0, split))):
-            nc.vector.quantize_mx(
-                out=h_codes[:, cols].bitcast(FP8X4),
-                scales=h_scale[:, cols],
-                in_=rounded[:].rearrange("p r m j -> p (r m j)"),
-            )
 
         spread_banks = ps.tile([P, 6, PACK, P], F32, name="own_spread", offset=0)
         own_spread = spread_banks[:, 0]
         for r in range(PACK):
             nc.tensor.transpose(own_spread[:, r, :], own_cols[:, r : r + 1].to_broadcast([P, P]), identity[:])
-        own_rows = shared.tile([P, PACK, P], F32, name="own_rows", offset=SPREAD_AT, align_bytes=64)
-        nc.scalar.activation(own_rows[:], own_spread, ACT.Copy, scale=-2.0 / 3.0)
+        own_rows = sb.tile([P, PACK, P], F32, name="own_rows", align_bytes=64)
+        nc.scalar.activation(own_rows[:], own_spread, ACT.Copy, scale=factor[:, 0:1])
 
         def lay_own(b, bank):
             laid = ps.tile([P, PACK, P], F32, name="turned%d" % b, offset=BANK * (bank))
@@ -151,7 +131,29 @@ def tile_picked_yrwmd_dist_p_kernel(
                 )
             return laid
 
-        turned = [lay_own(0, 6)]
+        turned = [lay_own(b, 6 + b) for b in range(BLOCKS)]
+
+        h_codes = sb.tile([P, V], U32, name="h_codes", align_bytes=64)
+        h_scale = sb.tile([P, V], U8, name="h_scale", align_bytes=64)
+        shares = (
+            (slice(SPLIT, V), SCALAR_ROUNDED_AT, nc.scalar.copy),
+            (slice(0, SPLIT), VECTOR_ROUNDED_AT, nc.vector.tensor_copy),
+        )
+        rounded = []
+        for cols, place, copy in shares:
+            name = "h_bf%d" % cols.start
+            h_bf = shared.tile([P, cols.stop - cols.start, PACK], BF16, name=name, offset=place, align_bytes=64)
+            copy(
+                h_bf[:].rearrange("p (m r) j -> p m j r", r=PACK),
+                h_raw[:, :, cols].rearrange("p j (m r) -> p m j r", r=PACK),
+            )
+            rounded.append(h_bf)
+        for (cols, place, copy), h_bf in zip(shares, rounded):
+            nc.vector.quantize_mx(
+                out=h_codes[:, cols].bitcast(FP8X4),
+                scales=h_scale[:, cols],
+                in_=h_bf[:].rearrange("p t j -> p (t j)"),
+            )
 
         x_codes = []
         for b in range(BLOCKS):
@@ -172,7 +174,7 @@ def tile_picked_yrwmd_dist_p_kernel(
         nc.gpsimd.tensor_tensor(idf_squared[:], idf_cols[:], idf_cols[:], ALU.mult)
 
         shift.append(
-            gather_norms(1, shared.tile([P, D * P], F32, name="second_norms", offset=NORMS_AT, align_bytes=64))
+            gather_norms(1, shared.tile([P, D * P], F32, name="second_norms", offset=RAW_AT, align_bytes=64))
         )
 
         bag_bf = shared.tile([P, N, PACK], BF16, name="bag_bf", offset=WORDS_AT, align_bytes=64)
@@ -197,58 +199,53 @@ def tile_picked_yrwmd_dist_p_kernel(
             )
             return acc
 
-        halves = (slice(0, HALF), slice(HALF, V))
-        for b in range(BLOCKS):
-            if b == 0:
-                opening = [
-                    multiply(0, 0, halves[0], DOT_BANKS[0][0])[:],
-                    multiply(0, 0, halves[1], DOT_BANKS[1][0])[:],
-                ]
-            else:
-                whole = multiply(b, 0, slice(0, V), DOT_BANKS[b][0])
-                opening = [whole[:, cols] for cols in halves]
-            dots = [None] + [multiply(b, d, slice(0, V), DOT_BANKS[b][d]) for d in range(1, D)]
-            run = []
-            for half in range(2):
-                tag = "run%d_0_%d" % (b, half)
-                first = sb.tile([P, HALF], F32, name="run%d_0_%d" % (b, half), tag=tag, align_bytes=64)
-                nc.scalar.activation(first[:], opening[half], ACT.Identity, bias=shift[b][:, 0:1])
-                run.append(first)
-            for d in range(1, D - 1):
-                for half in range(2):
-                    name = "run%d_%d_%d" % (b, d, half)
-                    tag = "run0_2_%d" % half if (b, d) == (1, 1) else name
-                    nxt = sb.tile([P, HALF], F32, name=name, tag=tag, align_bytes=64)
-                    nc.vector.scalar_tensor_tensor(
-                        nxt[:],
-                        dots[d][:, half * HALF : (half + 1) * HALF],
-                        shift[b][:, d : d + 1],
-                        run[half][:],
-                        ALU.add,
-                        ALU.max,
-                    )
-                    run[half] = nxt
-            slots = []
-            for lo, hi in (((0, 2), (2, 4)), ((0, 2), (2, 3), (3, 4)))[b]:
-                if (b, lo) == (0, 2):
-                    last = shared.tile([P, 2, P], F32, name="best0_2", offset=NORMS_AT, align_bytes=64)
-                else:
-                    last = sb.tile([P, hi - lo, P], F32, name="best%d_%d" % (b, lo))
-                nc.vector.scalar_tensor_tensor(
-                    last[:].rearrange("p r m -> p (r m)"),
-                    dots[D - 1][:, lo * P : hi * P],
-                    shift[b][:, D - 1 : D],
-                    run[lo // 2][:, (lo % 2) * P : (lo % 2 + hi - lo) * P],
-                    ALU.add,
-                    ALU.max,
-                )
-                slots.extend(last[:, i, :] for i in range(hi - lo))
+        def by_slot(columns):
+            return columns.rearrange("p (m r) -> p r m", r=PACK)
+
+        def open_run(name, b, dots):
+            first = sb.tile([P] + list(dots.shape[1:]), F32, name=name, tag=name, align_bytes=64)
+            nc.scalar.activation(first[:], dots, ACT.Identity, bias=shift[b][:, 0:1])
+            return first[:]
+
+        def step(target, b, d, dots, run):
+            nc.vector.scalar_tensor_tensor(target, dots, shift[b][:, d : d + 1], run, ALU.add, ALU.max)
+            return target
+
+        def fresh(name, shape, tag=None):
+            return sb.tile([P] + shape, F32, name=name, tag=tag or name, align_bytes=64)[:]
+
+        def turn(b, slots):
             for r in range(PACK):
                 nc.tensor.matmul(
                     turned[b][:, r, :], slots[r], identity[:], start=False, stop=(r == PACK - 1), is_transpose=True
                 )
-            if b == 0:
-                turned.append(lay_own(1, DOT_BANKS[0][D - 1]))
+
+        halves = (slice(0, HALF), slice(HALF, V))
+        opening = [multiply(0, 0, halves[u], DOT_BANKS[u][0])[:] for u in range(2)]
+        dots = [None] + [multiply(0, d, slice(0, V), DOT_BANKS[0][d]) for d in range(1, D)]
+        runs = [open_run("run0_0_%d" % u, 0, by_slot(opening[u])) for u in range(2)]
+        for d in range(1, D - 1):
+            for u in range(2):
+                target = fresh("run0_%d_%d" % (d, u), [PACK, P // 2])
+                runs[u] = step(target, 0, d, by_slot(dots[d][:, halves[u]]), runs[u])
+        best = shared.tile([P, PACK, P], F32, name="best0", offset=RAW_AT, align_bytes=64)
+        for u in range(2):
+            target = best[:, :, u * (P // 2) : (u + 1) * (P // 2)]
+            step(target, 0, D - 1, by_slot(dots[D - 1][:, halves[u]]), runs[u])
+        turn(0, [best[:, r, :] for r in range(PACK)])
+
+        dots = [by_slot(multiply(1, d, slice(0, V), DOT_BANKS[1][d])[:]) for d in range(D)]
+        runs = [open_run("run1_0_%d" % u, 1, dots[0][:, 2 * u : 2 * u + 2, :]) for u in range(2)]
+        for d in range(1, D - 1):
+            for u in range(2):
+                target = fresh("run1_%d_%d" % (d, u), [2, P], "run0_2_%d" % u if d == 1 else None)
+                runs[u] = step(target, 1, d, dots[d][:, 2 * u : 2 * u + 2, :], runs[u])
+        slots = []
+        for lo, hi in ((0, 2), (2, 3), (3, 4)):
+            run = runs[lo // 2][:, lo % 2 : lo % 2 + hi - lo, :]
+            last = step(fresh("best1_%d" % lo, [hi - lo, P]), 1, D - 1, dots[D - 1][:, lo:hi, :], run)
+            slots.extend(last[:, i, :] for i in range(hi - lo))
+        turn(1, slots)
 
         z_bf = [sb.tile([P, P, PACK], BF16, name="z_bf%d" % b, align_bytes=64) for b in range(BLOCKS)]
 
@@ -320,7 +317,7 @@ def tile_picked_yrwmd_dist_p_kernel(
         nc.scalar.copy(result[:], sums[:])
         nc.sync.dma_start(out.rearrange("(a p) g -> p a g", p=P)[:, :, 0:P], result[:])
 
-        upper = ps.tile([P, P], F32, name="sums_upper", offset=BANK * 7)
+        upper = ps.tile([P, P], F32, name="sums_upper", offset=BANK * 3)
         weigh(upper[:], 0, 1)
         lower = ps.tile([P, P], F32, name="sums_lower", offset=BANK * 4)
         weigh(lower[:], 1, 1)

@@ -173,6 +173,9 @@ def tile_picked_yrwmd_dist_p_kernel(
         idf_squared = shared.tile([P, PACK], F32, name="idf_squared", offset=SIGNS_AT + 64, align_bytes=64)
         nc.gpsimd.tensor_tensor(idf_squared[:], idf_cols[:], idf_cols[:], ALU.mult)
 
+        floor = sb.tile([P, PACK], F32, name="floor")
+        nc.gpsimd.tensor_scalar(floor[:], idf_squared[:], EPS, 0.0, ALU.mult, ALU.add)
+
         shift.append(
             gather_norms(1, shared.tile([P, D * P], F32, name="second_norms", offset=RAW_AT, align_bytes=64))
         )
@@ -249,15 +252,24 @@ def tile_picked_yrwmd_dist_p_kernel(
 
         z_bf = [sb.tile([P, P, PACK], BF16, name="z_bf%d" % b, align_bytes=64) for b in range(BLOCKS)]
 
-        def root_without_vector(b, docs):
-            clipped = sb.tile([P, 64, PACK], F32, name="clipped_early", align_bytes=64)
-            near = sb.tile([P, 64, PACK], F32, name="near", align_bytes=64)
+        clipped_first = sb.tile([P, PACK, P], F32, name="clipped_first", align_bytes=64)
+        near = sb.tile([P, 64, PACK], F32, name="near", align_bytes=64)
+        for docs in (slice(0, 64), slice(64, P)):
+            nc.scalar.activation(clipped_first[:, :, docs], turned[0][:, :, docs], ACT.Relu, scale=-1.5, bias=-EPS)
+            if docs.start == 0:
+                nc.scalar.activation(
+                    near[:], clipped_first[:, :, docs].rearrange("p r g -> p g r"), ACT.Sqrt, bias=eps[:]
+                )
+        nc.gpsimd.tensor_tensor(
+            z_bf[0][:, 0:64, :], near[:], idf_size[:].unsqueeze(1).to_broadcast([P, 64, PACK]), ALU.mult
+        )
+        for r in range(PACK):
             nc.scalar.activation(
-                clipped[:], turned[b][:, :, docs].rearrange("p r g -> p g r"), ACT.Relu, scale=-1.5, bias=-EPS
-            )
-            nc.scalar.activation(near[:], clipped[:], ACT.Sqrt, bias=eps[:])
-            nc.gpsimd.tensor_tensor(
-                z_bf[b][:, docs, :], near[:], idf_size[:].unsqueeze(1).to_broadcast([P, 64, PACK]), ALU.mult
+                z_bf[0][:, 64:P, r],
+                clipped_first[:, r, 64:P],
+                ACT.Sqrt,
+                scale=idf_squared[:, r : r + 1],
+                bias=floor[:, r : r + 1],
             )
 
         def root_with_vector(b, docs, tag):
@@ -272,9 +284,7 @@ def tile_picked_yrwmd_dist_p_kernel(
             )
             nc.scalar.activation(z_bf[b][:, docs, :], clipped[:], ACT.Sqrt, scale=-1.5)
 
-        root_without_vector(0, slice(0, 64))
-        root_with_vector(0, slice(64, P), "member_norms1")
-        bag_codes = sb.tile([P, N], U32, name="bag_codes", tag="run1_2_1", align_bytes=64)
+        bag_codes = sb.tile([P, N], U32, name="bag_codes", tag="member_norms1", align_bytes=64)
         bag_scale = sb.tile([P, N], U8, name="bag_scale", align_bytes=64)
         nc.vector.quantize_mx(
             out=bag_codes[:].bitcast(FP8X4),

@@ -8,11 +8,11 @@ P = 128
 PACK = 4
 G = S // D
 BLOCKS = G // P
-HALF = V // 2
 EPS = 0.01
 SCALE_ROWS = 16
 CLEARED = T // 2
 SPLIT = 3 * V // 4
+WEIGHED = P // 4
 IDF_AT = 4 * PACK * N
 SCALES_AT = IDF_AT - 64
 VECTOR_ROUNDED_AT = SCALES_AT + T - 64
@@ -23,7 +23,7 @@ WORDS_AT = CODES_AT + 4 * S
 SIGNS_AT = WORDS_AT + 2 * PACK * N
 RAW_AT = WORDS_AT + 4 * T
 BANK = 2048
-DOT_BANKS = ((0, 1, 2, 3), (4, 5, 0, 1))
+DOT_BANKS = ((0, 1, 2, 3), (4, 5, 0, 3))
 
 F32 = mybir.dt.float32
 BF16 = mybir.dt.bfloat16
@@ -223,50 +223,39 @@ def tile_picked_yrwmd_dist_p_kernel(
                     turned[b][:, r, :], slots[r], identity[:], start=False, stop=(r == PACK - 1), is_transpose=True
                 )
 
-        halves = (slice(0, HALF), slice(HALF, V))
-        opening = [multiply(0, 0, halves[u], DOT_BANKS[u][0])[:] for u in range(2)]
-        dots = [None] + [multiply(0, d, slice(0, V), DOT_BANKS[0][d]) for d in range(1, D)]
-        runs = [open_run("run0_0_%d" % u, 0, by_slot(opening[u])) for u in range(2)]
-        for d in range(1, D - 1):
-            for u in range(2):
-                target = fresh("run0_%d_%d" % (d, u), [PACK, P // 2])
-                runs[u] = step(target, 0, d, by_slot(dots[d][:, halves[u]]), runs[u])
-        best = shared.tile([P, PACK, P], F32, name="best0", offset=RAW_AT, align_bytes=64)
-        for u in range(2):
-            target = best[:, :, u * (P // 2) : (u + 1) * (P // 2)]
-            step(target, 0, D - 1, by_slot(dots[D - 1][:, halves[u]]), runs[u])
-        turn(0, [best[:, r, :] for r in range(PACK)])
-
-        dots = [by_slot(multiply(1, d, slice(0, V), DOT_BANKS[1][d])[:]) for d in range(D)]
-        runs = [open_run("run1_0_%d" % u, 1, dots[0][:, 2 * u : 2 * u + 2, :]) for u in range(2)]
-        for d in range(1, D - 1):
-            for u in range(2):
-                target = fresh("run1_%d_%d" % (d, u), [2, P], "run0_2_%d" % u if d == 1 else None)
-                runs[u] = step(target, 1, d, dots[d][:, 2 * u : 2 * u + 2, :], runs[u])
-        slots = []
-        for lo, hi in ((0, 2), (2, 3), (3, 4)):
-            run = runs[lo // 2][:, lo % 2 : lo % 2 + hi - lo, :]
-            last = step(fresh("best1_%d" % lo, [hi - lo, P]), 1, D - 1, dots[D - 1][:, lo:hi, :], run)
-            slots.extend(last[:, i, :] for i in range(hi - lo))
-        turn(1, slots)
+        for b, pieces in enumerate((((0, 2), (2, 4)), ((0, 2), (2, 3), (3, 4)))):
+            dots = [by_slot(multiply(b, d, slice(0, V), DOT_BANKS[b][d])[:]) for d in range(D)]
+            runs = [open_run("run%d_0_%d" % (b, u), b, dots[0][:, 2 * u : 2 * u + 2, :]) for u in range(2)]
+            for d in range(1, D - 1):
+                for u in range(2):
+                    target = fresh("run%d_%d_%d" % (b, d, u), [2, P], "run0_2_%d" % u if (b, d) == (1, 1) else None)
+                    runs[u] = step(target, b, d, dots[d][:, 2 * u : 2 * u + 2, :], runs[u])
+            slots = []
+            for lo, hi in pieces:
+                if (b, lo) == (0, 2):
+                    target = shared.tile([P, 2, P], F32, name="best0_2", offset=RAW_AT, align_bytes=64)[:]
+                else:
+                    target = fresh("best%d_%d" % (b, lo), [hi - lo, P])
+                run = runs[lo // 2][:, lo % 2 : lo % 2 + hi - lo, :]
+                last = step(target, b, D - 1, dots[D - 1][:, lo:hi, :], run)
+                slots.extend(last[:, i, :] for i in range(hi - lo))
+            turn(b, slots)
 
         z_bf = [sb.tile([P, P, PACK], BF16, name="z_bf%d" % b, align_bytes=64) for b in range(BLOCKS)]
 
         clipped_first = sb.tile([P, PACK, P], F32, name="clipped_first", align_bytes=64)
-        near = sb.tile([P, 64, PACK], F32, name="near", align_bytes=64)
-        for docs in (slice(0, 64), slice(64, P)):
-            nc.scalar.activation(clipped_first[:, :, docs], turned[0][:, :, docs], ACT.Relu, scale=-1.5, bias=-EPS)
-            if docs.start == 0:
-                nc.scalar.activation(
-                    near[:], clipped_first[:, :, docs].rearrange("p r g -> p g r"), ACT.Sqrt, bias=eps[:]
-                )
+        near = sb.tile([P, WEIGHED, PACK], F32, name="near", align_bytes=64)
+        nc.scalar.activation(clipped_first[:], turned[0][:], ACT.Relu, scale=-1.5, bias=-EPS)
+        nc.scalar.activation(
+            near[:], clipped_first[:, :, 0:WEIGHED].rearrange("p r g -> p g r"), ACT.Sqrt, bias=eps[:]
+        )
         nc.gpsimd.tensor_tensor(
-            z_bf[0][:, 0:64, :], near[:], idf_size[:].unsqueeze(1).to_broadcast([P, 64, PACK]), ALU.mult
+            z_bf[0][:, 0:WEIGHED, :], near[:], idf_size[:].unsqueeze(1).to_broadcast([P, WEIGHED, PACK]), ALU.mult
         )
         for r in range(PACK):
             nc.scalar.activation(
-                z_bf[0][:, 64:P, r],
-                clipped_first[:, r, 64:P],
+                z_bf[0][:, WEIGHED:P, r],
+                clipped_first[:, r, WEIGHED:P],
                 ACT.Sqrt,
                 scale=idf_squared[:, r : r + 1],
                 bias=floor[:, r : r + 1],
@@ -327,7 +316,7 @@ def tile_picked_yrwmd_dist_p_kernel(
         nc.scalar.copy(result[:], sums[:])
         nc.sync.dma_start(out.rearrange("(a p) g -> p a g", p=P)[:, :, 0:P], result[:])
 
-        upper = ps.tile([P, P], F32, name="sums_upper", offset=BANK * 3)
+        upper = ps.tile([P, P], F32, name="sums_upper", offset=BANK * 1)
         weigh(upper[:], 0, 1)
         lower = ps.tile([P, P], F32, name="sums_lower", offset=BANK * 4)
         weigh(lower[:], 1, 1)

from contextlib import ExitStack

import concourse.mybir as mybir
from concourse.masks import make_identity

K, T, S, V, D, N = 512, 2048, 1024, 512, 4, 256
P = 128
PACK = 4
G = S // D
BLOCKS = G // P
EPS = 0.01
SCALE_ROWS = 16
CLEARED = T // 2
SPLIT = 3 * V // 4
WEIGHED = P // 4
IDF_AT = 4 * PACK * N
SCALES_AT = IDF_AT - 64
VECTOR_ROUNDED_AT = SCALES_AT + T - 64
SCALAR_ROUNDED_AT = VECTOR_ROUNDED_AT + 2 * PACK * SPLIT
FACTOR_AT = SCALAR_ROUNDED_AT + 64
CODES_AT = SCALAR_ROUNDED_AT + PACK * (V - SPLIT) - 4 * D * P
WORDS_AT = CODES_AT + 4 * S
SIGNS_AT = WORDS_AT + 2 * PACK * N
RAW_AT = WORDS_AT + 4 * T
BANK = 2048
DOT_BANKS = ((0, 1, 2, 3), (4, 5, 0, 3))

F32 = mybir.dt.float32
BF16 = mybir.dt.bfloat16
I32 = mybir.dt.int32
U32 = mybir.dt.uint32
U16 = mybir.dt.uint16
U8 = mybir.dt.uint8
FP8X4 = mybir.dt.float8_e4m3fn_x4
ALU = mybir.AluOpType
ACT = mybir.ActivationFunctionType

FLOPS = 2 * K * V * S + 2 * V * N * G
BYTES = K * T + 16 * T + 4 * (K * V + T + 2 * V + V * N + N * G) + 2 * P * (S // 16)


def tile_picked_yrwmd_dist_p_kernel(
    tc, x_words, x_scales, hT, qn, own, idf, bag, offs, out
):
    nc = tc.nc
    with ExitStack() as ctx:
        sb = ctx.enter_context(tc.tile_pool(name="sb", bufs=1))
        shared = ctx.enter_context(tc.tile_pool(name="shared", bufs=1))
        ps = ctx.enter_context(tc.psum_pool(name="ps", bufs=1))

        offsets = sb.tile([P, S // 16], U16, name="offsets")
        nc.sync.dma_start(offsets[:], offs)

        norm_table = sb.tile([P, T], F32, name="norm_table", align_bytes=64)
        nc.scalar.dma_start(norm_table[P - 1 : P, :], qn[0:1, :])
        scale_table = shared.tile([P, T], U8, name="scale_table", offset=SCALES_AT, align_bytes=64)
        nc.sync.dma_start(scale_table[P - SCALE_ROWS : P, :].bitcast(I32), x_scales[0].bitcast(I32))
        own_cols = sb.tile([P, PACK], F32, name="own_cols")
        nc.sync.dma_start(own_cols[:], own.rearrange("(p j) o -> p (j o)", j=PACK))
        h_raw = shared.tile([P, PACK, V], F32, name="h_raw", offset=RAW_AT, align_bytes=64)
        nc.sync.dma_start(h_raw[:], hT.rearrange("(p j) t -> p j t", j=PACK))
        word_table = shared.tile([P, T], U32, name="word_table", offset=WORDS_AT, align_bytes=64)
        nc.sync.dma_start(
            word_table[:].bitcast(I32),
            x_words[0].rearrange("p c r -> p (c r)").bitcast(I32),
        )

        one = sb.tile([P, 1], F32, name="one")
        nc.gpsimd.memset(one[:], 1.0)
        nc.vector.memset(norm_table[0 : P - 1, 0 : CLEARED - 1], 0.0)
        nc.vector.memset(norm_table[0 : P - 1, CLEARED - 1 : CLEARED], 0.0)
        nc.gpsimd.memset(scale_table[0 : P - SCALE_ROWS, :].bitcast(I32), 0)
        nc.gpsimd.memset(norm_table[0 : P - 1, CLEARED:T], 0.0)
        eps = sb.tile([P, 1], F32, name="eps")
        nc.scalar.activation(eps[:], one[:], ACT.Sqrt, scale=EPS * EPS)
        identity = sb.tile([P, P], F32, name="identity")
        make_identity(nc, identity[:])
        factor = shared.tile([P, 16], F32, name="factor", offset=FACTOR_AT, align_bytes=64)
        nc.gpsimd.tensor_scalar(factor[:, 0:1], one[:], -2.0 / 3.0, 0.0, ALU.mult, ALU.add)
        planes = sb.tile([P, S], U8, name="x_scale", align_bytes=64)
        nc.vector.memset(planes[:].bitcast(I32), 0)
        x_scale = [planes[:, b * D * P : (b + 1) * D * P] for b in range(BLOCKS)]
        ceiling = sb.tile([P, 1], F32, name="ceiling")
        nc.gpsimd.tensor_scalar(ceiling[:], one[:], -EPS / 1.5, 0.0, ALU.mult, ALU.add)

        def move_norms(b, picked_norms):
            name = "member_norms%d" % b
            member_norms = sb.tile([P, D], F32, name=name, tag=name, align_bytes=64)
            nc.sync.dma_start(member_norms[:], picked_norms[P - 1 : P, :].rearrange("o (g d) -> o g d", d=D))
            return member_norms

        def gather_norms(b, picked_norms):
            nc.scalar.activation(
                picked_norms[:],
                norm_table[:].indirect(offsets[:, 32 * b : 32 * (b + 1)]),
                ACT.Copy,
                scale=-2.0 / 3.0,
                bias=-EPS / 1.5,
            )
            return move_norms(b, picked_norms)

        shift = [gather_norms(0, sb.tile([P, D * P], F32, name="first_norms", align_bytes=64))]

        picked_scales = sb.tile([P, BLOCKS, D, P], U8, name="picked_scales", align_bytes=64)
        nc.vector.tensor_copy(
            picked_scales[:].rearrange("p b d g -> p b g d"), scale_table[:].indirect(offsets[:])
        )
        for q in range(4):
            rows = slice(P - SCALE_ROWS + 4 * q, P - SCALE_ROWS + 4 * q + 4)
            nc.sync.dma_start(
                planes[32 * q : 32 * q + 4, :].bitcast(I32),
                picked_scales[rows].rearrange("p b d g -> p (b d g)").bitcast(I32),
            )
        bag_raw = shared.tile([P, PACK, N], F32, name="bag_raw", offset=0, align_bytes=64)
        nc.sync.dma_start(bag_raw[:], bag.rearrange("(p j) m -> p j m", j=PACK))
        idf_cols = shared.tile([P, PACK], F32, name="idf_cols", offset=IDF_AT, align_bytes=64)
        nc.sync.dma_start(idf_cols[:], idf.rearrange("(p j) o -> p (j o)", j=PACK))

        spread_banks = ps.tile([P, 6, PACK, P], F32, name="own_spread", offset=0)
        own_spread = spread_banks[:, 0]
        for r in range(PACK):
            nc.tensor.transpose(own_spread[:, r, :], own_cols[:, r : r + 1].to_broadcast([P, P]), identity[:])
        own_rows = sb.tile([P, PACK, P], F32, name="own_rows", align_bytes=64)
        nc.scalar.activation(own_rows[:], own_spread, ACT.Copy, scale=factor[:, 0:1])

        def lay_own(b, bank):
            laid = ps.tile([P, PACK, P], F32, name="turned%d" % b, offset=BANK * (bank))
            for r in range(PACK):
                nc.tensor.matmul(
                    laid[:, r, :], own_rows[:, r, :], identity[:], start=(r == 0), stop=False, is_transpose=True
                )
            return laid

        turned = [lay_own(b, 6 + b) for b in range(BLOCKS)]

        h_codes = sb.tile([P, V], U32, name="h_codes", align_bytes=64)
        h_scale = sb.tile([P, V], U8, name="h_scale", align_bytes=64)
        shares = (
            (slice(SPLIT, V), SCALAR_ROUNDED_AT, nc.scalar.copy),
            (slice(0, SPLIT), VECTOR_ROUNDED_AT, nc.vector.tensor_copy),
        )
        rounded = []
        for cols, place, copy in shares:
            name = "h_bf%d" % cols.start
            h_bf = shared.tile([P, cols.stop - cols.start, PACK], BF16, name=name, offset=place, align_bytes=64)
            copy(
                h_bf[:].rearrange("p (m r) j -> p m j r", r=PACK),
                h_raw[:, :, cols].rearrange("p j (m r) -> p m j r", r=PACK),
            )
            rounded.append(h_bf)
        for (cols, place, copy), h_bf in zip(shares, rounded):
            nc.vector.quantize_mx(
                out=h_codes[:, cols].bitcast(FP8X4),
                scales=h_scale[:, cols],
                in_=h_bf[:].rearrange("p t j -> p (t j)"),
            )

        x_codes = []
        for b in range(BLOCKS):
            codes = shared.tile([P, D, P], U32, name="x_codes%d" % b, offset=CODES_AT + 4 * D * P * b, align_bytes=64)
            nc.vector.tensor_copy(
                codes[:].rearrange("p d g -> p g d"),
                word_table[:].indirect(offsets[:, 32 * b : 32 * (b + 1)]),
            )
            x_codes.append(codes)

        idf_positive = shared.tile([P, PACK], F32, name="idf_positive", offset=SIGNS_AT, align_bytes=64)
        nc.gpsimd.tensor_scalar(idf_positive[:], idf_cols[:], 0.0, None, ALU.is_ge)
        idf_sign = sb.tile([P, PACK], F32, name="idf_sign")
        nc.gpsimd.tensor_scalar(idf_sign[:], idf_positive[:], 2.0, -1.0, ALU.mult, ALU.add)
        idf_size = sb.tile([P, PACK], F32, name="idf_size")
        nc.gpsimd.tensor_tensor(idf_size[:], idf_cols[:], idf_sign[:], ALU.mult)
        idf_squared = shared.tile([P, PACK], F32, name="idf_squared", offset=SIGNS_AT + 64, align_bytes=64)
        nc.gpsimd.tensor_tensor(idf_squared[:], idf_cols[:], idf_cols[:], ALU.mult)

        floor = sb.tile([P, PACK], F32, name="floor")
        nc.gpsimd.tensor_scalar(floor[:], idf_squared[:], EPS, 0.0, ALU.mult, ALU.add)

        shift.append(
            gather_norms(1, shared.tile([P, D * P], F32, name="second_norms", offset=RAW_AT, align_bytes=64))
        )

        bag_bf = shared.tile([P, N, PACK], BF16, name="bag_bf", offset=WORDS_AT, align_bytes=64)
        nc.gpsimd.tensor_tensor(
            bag_bf[:],
            bag_raw[:].rearrange("p j m -> p m j"),
            idf_sign[:].unsqueeze(1).to_broadcast([P, N, PACK]),
            ALU.mult,
        )

        def multiply(b, d, cols, bank):
            name = "dots%d_%d_%d" % (b, d, cols.start)
            acc = ps.tile([P, cols.stop - cols.start], F32, name=name, offset=BANK * (bank))
            nc.tensor.matmul_mx(
                out=acc[:],
                lhsT=x_codes[b][:, d, :].bitcast(FP8X4),
                lhsT_scale=x_scale[b][:, P * d : P * (d + 1)],
                rhs=h_codes[:, cols].bitcast(FP8X4),
                rhs_scale=h_scale[:, cols],
                start=True,
                stop=True,
            )
            return acc

        def by_slot(columns):
            return columns.rearrange("p (m r) -> p r m", r=PACK)

        def open_run(name, b, dots):
            first = sb.tile([P] + list(dots.shape[1:]), F32, name=name, tag=name, align_bytes=64)
            nc.scalar.activation(first[:], dots, ACT.Identity, bias=shift[b][:, 0:1])
            return first[:]

        def step(target, b, d, dots, run):
            nc.vector.scalar_tensor_tensor(target, dots, shift[b][:, d : d + 1], run, ALU.add, ALU.max)
            return target

        def fresh(name, shape, tag=None):
            return sb.tile([P] + shape, F32, name=name, tag=tag or name, align_bytes=64)[:]

        def turn(b, slots):
            for r in range(PACK):
                nc.tensor.matmul(
                    turned[b][:, r, :], slots[r], identity[:], start=False, stop=(r == PACK - 1), is_transpose=True
                )

        for b, pieces in enumerate((((0, 2), (2, 4)), ((0, 2), (2, 3), (3, 4)))):
            dots = [by_slot(multiply(b, d, slice(0, V), DOT_BANKS[b][d])[:]) for d in range(D)]
            runs = [open_run("run%d_0_%d" % (b, u), b, dots[0][:, 2 * u : 2 * u + 2, :]) for u in range(2)]
            for d in range(1, D - 1):
                for u in range(2):
                    target = fresh("run%d_%d_%d" % (b, d, u), [2, P], "run0_2_%d" % u if (b, d) == (1, 1) else None)
                    runs[u] = step(target, b, d, dots[d][:, 2 * u : 2 * u + 2, :], runs[u])
            slots = []
            for lo, hi in pieces:
                if (b, lo) == (0, 2):
                    target = shared.tile([P, 2, P], F32, name="best0_2", offset=RAW_AT, align_bytes=64)[:]
                else:
                    target = fresh("best%d_%d" % (b, lo), [hi - lo, P])
                run = runs[lo // 2][:, lo % 2 : lo % 2 + hi - lo, :]
                last = step(target, b, D - 1, dots[D - 1][:, lo:hi, :], run)
                slots.extend(last[:, i, :] for i in range(hi - lo))
            turn(b, slots)

        z_bf = [sb.tile([P, P, PACK], BF16, name="z_bf%d" % b, align_bytes=64) for b in range(BLOCKS)]

        clipped_first = sb.tile([P, PACK, P], F32, name="clipped_first", align_bytes=64)
        near = sb.tile([P, WEIGHED, PACK], F32, name="near", align_bytes=64)
        nc.scalar.activation(clipped_first[:], turned[0][:], ACT.Relu, scale=-1.5, bias=-EPS)
        nc.scalar.activation(
            near[:], clipped_first[:, :, 0:WEIGHED].rearrange("p r g -> p g r"), ACT.Sqrt, bias=eps[:]
        )
        nc.gpsimd.tensor_tensor(
            z_bf[0][:, 0:WEIGHED, :], near[:], idf_size[:].unsqueeze(1).to_broadcast([P, WEIGHED, PACK]), ALU.mult
        )
        for r in range(PACK):
            nc.scalar.activation(
                z_bf[0][:, WEIGHED:P, r],
                clipped_first[:, r, WEIGHED:P],
                ACT.Sqrt,
                scale=idf_squared[:, r : r + 1],
                bias=floor[:, r : r + 1],
            )

        def root_with_vector(b, docs, tag):
            clipped = sb.tile([P, 64, PACK], F32, name="clipped%d_%d" % (b, docs.start), tag=tag, align_bytes=64)
            nc.vector.scalar_tensor_tensor(
                clipped[:],
                turned[b][:, :, docs].rearrange("p r g -> p g r"),
                ceiling[:],
                idf_squared[:].unsqueeze(1).to_broadcast([P, 64, PACK]),
                ALU.min,
                ALU.mult,
            )
            nc.scalar.activation(z_bf[b][:, docs, :], clipped[:], ACT.Sqrt, scale=-1.5)

        bag_codes = sb.tile([P, N], U32, name="bag_codes", tag="member_norms1", align_bytes=64)
        bag_scale = sb.tile([P, N], U8, name="bag_scale", align_bytes=64)
        nc.vector.quantize_mx(
            out=bag_codes[:].bitcast(FP8X4),
            scales=bag_scale[:],
            in_=bag_bf[:].rearrange("p m j -> p (m j)"),
        )

        root_with_vector(1, slice(0, 64), "clipped_upper")
        root_with_vector(1, slice(64, P), "clipped_lower")

        z_mx = []
        for b in range(BLOCKS):
            if b == 0:
                z_codes = shared.tile([P, P], U32, name="z_codes0", offset=SIGNS_AT + 64, align_bytes=64)
            else:
                z_codes = sb.tile([P, P], U32, name="z_codes1", align_bytes=64)
            z_scale = sb.tile([P, P], U8, name="z_scale%d" % b, align_bytes=64)
            nc.vector.quantize_mx(
                out=z_codes[:].bitcast(FP8X4),
                scales=z_scale[:],
                in_=z_bf[b][:].rearrange("p g r -> p (g r)"),
            )
            z_mx.append((z_codes, z_scale))

        def weigh(target, a, b):
            nc.tensor.matmul_mx(
                out=target,
                lhsT=bag_codes[:, a * P : (a + 1) * P].bitcast(FP8X4),
                lhsT_scale=bag_scale[:, a * P : (a + 1) * P],
                rhs=z_mx[b][0][:].bitcast(FP8X4),
                rhs_scale=z_mx[b][1][:],
                start=True,
                stop=True,
            )

        sums = ps.tile([P, N // P, P], F32, name="sums_first", offset=BANK * 2)
        for a in range(N // P):
            weigh(sums[:, a, :], a, 0)
        result = sb.tile([P, N // P, P], F32, name="result_first")
        nc.scalar.copy(result[:], sums[:])
        nc.sync.dma_start(out.rearrange("(a p) g -> p a g", p=P)[:, :, 0:P], result[:])

        upper = ps.tile([P, P], F32, name="sums_upper", offset=BANK * 1)
        weigh(upper[:], 0, 1)
        lower = ps.tile([P, P], F32, name="sums_lower", offset=BANK * 4)
        weigh(lower[:], 1, 1)
        upper_result = sb.tile([P, P], F32, name="upper_result")
        nc.vector.tensor_copy(upper_result[:], upper[:])
        nc.sync.dma_start(out[0:P, P : 2 * P], upper_result[:])
        lower_result = sb.tile([P, P], F32, name="lower_result")
        nc.scalar.copy(lower_result[:], lower[:])
        nc.scalar.dma_start(out[P : 2 * P, P : 2 * P], lower_result[:])
